import numpy as np
import ml_dtypes


def mxq(x, axis, fmt="e4m3"):
    dtype, down = {"e4m3": (ml_dtypes.float8_e4m3fn, 7), "e5m2": (ml_dtypes.float8_e5m2, 14)}[fmt]
    v = np.moveaxis(np.asarray(x, np.float32).astype(ml_dtypes.bfloat16).astype(np.float64), axis, -1)
    blocks = v.reshape(v.shape[:-1] + (-1, 32))
    amax = np.abs(blocks).max(-1, keepdims=True)
    byte = np.maximum(np.where(amax > 0, np.frexp(amax)[1] - 1 + 127, 0) - down, 1)
    scale = np.exp2(byte - 127.0)
    codes = (blocks / scale).astype(np.float32).astype(dtype).astype(np.float64)
    return np.moveaxis((codes * scale).reshape(v.shape), -1, axis)


WIDE = False


def mx_kscale(k):
    if not WIDE:
        return np.ones(k)
    levels = np.array([10, -10, 5, -5, 0])
    if k % 512:
        return np.exp2(np.random.permutation(np.resize(levels, k // 32))).repeat(32)
    a = np.empty((k // 512, 16))
    for p in range(k // 512):
        a[p, :8] = np.random.permutation(np.resize(levels, 8))
        for g in range(8):
            far = levels[np.abs(levels - a[p, g]) >= 10]
            a[p, g + 8] = far[np.random.randint(len(far))]
    return np.exp2(a.ravel()).repeat(32)


def f64(x):
    return np.asarray(x).astype(np.float64)


def striped(idx):
    return np.tile(idx.reshape(-1, 16).T, (8, 1)).astype(np.uint16)


def unstriped(offs):
    return offs[:16].T.reshape(-1).astype(np.int64)


E2M1 = np.array([0.0, 0.5, 1.0, 1.5, 2.0, 3.0, 4.0, 6.0, -0.0, -0.5, -1.0, -1.5, -2.0, -3.0, -4.0, -6.0])


def pack_weight(w, fmt):
    k, n = w.shape
    w = f64(np.asarray(w, np.float32).astype(ml_dtypes.bfloat16)).reshape(k // 32, 32, n)
    amax = np.abs(w).max(1)
    if fmt == "e4m3":
        byte = np.frexp(amax)[1] - 1 + 127 - 7
    else:
        mant, ex = np.frexp(amax / 6.0)
        byte = np.where(mant > 0.5, ex, ex - 1) + 127
    byte = np.clip(np.where(amax > 0, byte, 1), 1, 254)
    scaled = (w * np.exp2(127.0 - byte)[:, None, :]).reshape(k, n).astype(np.float32)
    by_word = np.ascontiguousarray(scaled.reshape(k // 512, 128, 4, n).transpose(0, 1, 3, 2))
    if fmt == "e4m3":
        words = by_word.astype(ml_dtypes.float8_e4m3fn).view(np.uint8)
    else:
        c = by_word.astype(ml_dtypes.float4_e2m1fn).view(np.uint8) & 0xF
        words = (c[..., 0::2] | (c[..., 1::2] << 4)).reshape(k // 512, 128, 2 * n)
    return np.ascontiguousarray(words), np.ascontiguousarray(byte.astype(np.uint8).reshape(k // 512, 16, n))


def unpack_weight(words, scales, fmt):
    g, _, n = scales.shape
    words = np.ascontiguousarray(words).reshape(g, 128, n, -1)
    if fmt == "e4m3":
        vals = words.view(ml_dtypes.float8_e4m3fn).astype(np.float64)
    else:
        nib = np.empty((g, 128, n, 4), np.uint8)
        nib[..., 0::2] = words & 0xF
        nib[..., 1::2] = words >> 4
        vals = E2M1[nib]
    vals = vals * np.repeat(np.exp2(scales.astype(np.float64) - 127.0), 8, axis=1)[..., None]
    return vals.transpose(0, 1, 3, 2).reshape(g * 512, n)


def relu(v):
    return np.maximum(v, 0.0)


K, T, E, C, H, N = 2048, 1024, 2, 256, 512, 384


def by_expert(wq, xq):
    return np.concatenate([wq[e].T @ xq[:, e * C:(e + 1) * C] for e in range(E)], axis=1)


def setup_inputs():
    n = np.random.standard_normal
    s = mx_kscale(K)[:, None]
    u = mx_kscale(H)
    w1 = [pack_weight(m, "e2m1") for m in n((E, K, H)) / np.sqrt(K) / s[None] * u[None, None, :]]
    w2 = [pack_weight(m, "e2m1") for m in n((E, H, N)) / np.sqrt(H) / u[None, :, None]]
    return {
        "xT": (n((K, T)) * s).astype(np.float32),
        "xr": n((N, T)).astype(np.float32),
        "w1_words": np.stack([m[0] for m in w1]),
        "w1_scales": np.stack([m[1] for m in w1]),
        "w2_words": np.stack([m[0] for m in w2]),
        "w2_scales": np.stack([m[1] for m in w2]),
        "gate": np.tile(np.random.uniform(0.2, 1.0, E * C), (N, 1)).astype(np.float32),
        "offs": striped(np.random.permutation(T)[:E * C]),
    }


def reference(xT, xr, w1_words, w1_scales, w2_words, w2_scales, gate, offs):
    idx = unstriped(offs)
    w1 = np.stack([unpack_weight(w1_words[e], w1_scales[e], "e2m1") for e in range(E)])
    w2 = np.stack([unpack_weight(w2_words[e], w2_scales[e], "e2m1") for e in range(E)])
    xq = mxq(f64(xT)[:, idx], 0, "e4m3")
    h = relu(by_expert(w1, xq))
    y = by_expert(w2, mxq(h, 0, "e4m3"))
    out = f64(xr).copy()
    out[:, idx] += f64(gate) * y
    return out

@@ -1,0 +1,277 @@
+from contextlib import ExitStack
+
+import concourse.mybir as mybir
+from concourse.masks import make_identity
+
+K, T, E, C, H, N = 2048, 1024, 2, 256, 512, 384
+P = 128
+PACK = 4
+PASSES = K // (P * PACK)
+S = E * C
+U_TILES = S // P
+N_TILES = N // P
+
+FLOPS = 2 * S * (K * H + H * N)
+BYTES = 4 * (K * T + 2 * N * T + P * S) + E * (K * H + H * N) // 2 + E * (K * H + H * N) // 32 + 2 * P * S // 16
+
+F32 = mybir.dt.float32
+BF16 = mybir.dt.bfloat16
+U32 = mybir.dt.uint32
+I32 = mybir.dt.int32
+U16 = mybir.dt.uint16
+U8 = mybir.dt.uint8
+E4M3 = mybir.dt.float8_e4m3fn_x4
+E2M1 = mybir.dt.float4_e2m1fn_x4
+COPY = mybir.ActivationFunctionType.Copy
+RELU = mybir.ActivationFunctionType.Relu
+MULT = mybir.AluOpType.mult
+ADD = mybir.AluOpType.add
+
+LOADS = [(0, 0, 1024), (1, 0, 1024), (2, 0, 1024), (3, 0, 512), (3, 512, 256), (3, 768, 256)]
+PIECES = [(0, 0, 512, 0), (0, 512, 512, 512), (1, 0, 512, 304), (1, 512, 512, 304), (2, 0, 512, 256), (2, 512, 512, 304)] + [
+    (3, 0, 512, 416), (4, 512, 256, 200), (5, 768, 256, 120)]
+
+
+def tile_moe_res_mlp_relu_kernel(
+    tc, xT, xr, w1_words, w1_scales, w2_words, w2_scales, gate, offs, out
+):
+    nc = tc.nc
+    with ExitStack() as ctx:
+        keep = ctx.enter_context(tc.tile_pool(name="keep", bufs=1))
+        psum = ctx.enter_context(tc.psum_pool(name="psum", bufs=1))
+
+        groups = (slice(0, P), slice(P, 2 * P), slice(C, S))
+        sizes = [g.stop - g.start for g in groups]
+        offsets = keep.tile([P, S // 16], U16, name="offsets")
+        w1s = keep.tile([P, E, PASSES * H], U8, name="w1s", align_bytes=64)
+        w2s = keep.tile([P, E, N], U8, name="w2s", align_bytes=64)
+        w1 = keep.tile([P, E, PASSES, 2 * H], U8, name="w1", align_bytes=64)
+        w2 = keep.tile([P, E, 2 * N], U8, name="w2", align_bytes=64)
+        gates = keep.tile([P, S], F32, name="gates")
+        warm = keep.tile([P, 8], F32, name="warm")
+        ident = keep.tile([P, P], F32, name="ident", align_bytes=64)
+        xf = [keep.tile([P, PACK, x[2]], F32, name=f"xf{i}", align_bytes=64) for i, x in enumerate(LOADS)]
+        xb = [keep.tile([P, x[2], PACK], BF16, name=f"xb{i}", align_bytes=64) for i, x in enumerate(PIECES)]
+        words = [keep.tile([P, T], U32, name=f"words{s}", align_bytes=64) for s in range(PASSES)]
+        scales = [keep.tile([P, T], U8, name=f"scales{s}", align_bytes=64) for s in range(PASSES)]
+        gw = [keep.tile([P, S], U32, name=f"gw{s}", align_bytes=64) for s in range(PASSES)]
+        gs = [keep.tile([P, S], U8, name=f"gs{s}", align_bytes=64) for s in range(PASSES)]
+        h = [keep.tile([P, H], BF16, name=f"h{u}", align_bytes=64) for u in range(U_TILES)]
+        hg = [keep.tile([P, n, PACK], BF16, name=f"hg{g}", align_bytes=64) for g, n in enumerate(sizes)]
+        hq = [keep.tile([P, n], U32, name=f"hq{g}", align_bytes=64) for g, n in enumerate(sizes)]
+        hs = [keep.tile([P, n], U8, name=f"hs{g}", align_bytes=64) for g, n in enumerate(sizes)]
+        yv = [keep.tile([P, N_TILES, n], F32, name=f"yv{g}", align_bytes=64) for g, n in enumerate(sizes)]
+        ys = [keep.tile([P, N_TILES, n], F32, name=f"ys{g}", align_bytes=64) for g, n in enumerate(sizes)]
+        back = [keep.tile([P, T], F32, name=f"back{n}", align_bytes=64) for n in range(N_TILES)]
+        res = [keep.tile([P, T], F32, name=f"res{n}", align_bytes=64) for n in range(N_TILES)]
+
+        nc.vector.memset(w1s[:].rearrange("p e i -> p (e i)").bitcast(I32), 0)
+        nc.vector.memset(w2s[:].rearrange("p e i -> p (e i)").bitcast(I32), 0)
+        nc.vector.memset(warm[:], 0.0)
+        for n in range(N_TILES):
+            nc.vector.memset(back[n][:], 0.0)
+        for s in range(PASSES):
+            nc.gpsimd.memset(scales[s][:].bitcast(I32), 0)
+        make_identity(nc, ident[:])
+
+        nc.sync.dma_start(offsets[:], offs)
+
+        def load_x(i):
+            s, t0, width = LOADS[i]
+            rows = xT[s * P * PACK : (s + 1) * P * PACK, t0 : t0 + width]
+            nc.sync.dma_start(out=xf[i][:], in_=rows.rearrange("(p j) t -> p j t", j=PACK))
+
+        def load_w1(e, s0):
+            nc.sync.dma_start(
+                out=w1[:, e, s0 : s0 + 2, :].bitcast(I32),
+                in_=w1_words[e, s0 : s0 + 2, :, :].bitcast(I32).rearrange("s p b -> p s b"),
+            )
+
+        def load_w1_scales(queue, e):
+            rows = w1_scales[e].bitcast(I32)
+            for q in range(4):
+                queue.dma_start(
+                    out=w1s[32 * q : 32 * q + 4, e, :].bitcast(I32).rearrange("q (s i) -> q s i", s=PASSES),
+                    in_=rows[:, 4 * q : 4 * q + 4, :].rearrange("s q i -> q s i"),
+                )
+
+        load_w1_scales(nc.scalar, 0)
+        load_x(0)
+        load_x(1)
+        load_w1(0, 0)
+        load_x(2)
+        load_w1(0, 2)
+        load_x(3)
+        load_x(4)
+        load_w1_scales(nc.sync, 1)
+        load_w1(1, 0)
+        load_x(5)
+        nc.sync.dma_start(out=gates[:], in_=gate[0:P, :])
+        load_w1(1, 2)
+        nc.sync.dma_start(out=w2[:].bitcast(I32), in_=w2_words[:, 0, :, :].bitcast(I32).rearrange("e p b -> p e b"))
+        rows = w2_scales[:, 0, :, :].bitcast(I32)
+        for q in range(4):
+            nc.sync.dma_start(
+                out=w2s[32 * q : 32 * q + 4, :, :].bitcast(I32),
+                in_=rows[:, 4 * q : 4 * q + 4, :].rearrange("e q i -> q e i"),
+            )
+        for n in range(N_TILES):
+            nc.sync.dma_start(out=res[n][:], in_=xr[n * P : (n + 1) * P, :])
+
+        nc.scalar.activation(warm[:], warm[:], RELU)
+        acc = [psum.tile([P, H], F32, name=f"acc{u}", tag="acc", bufs=U_TILES) for u in range(U_TILES)]
+
+        def cast(i, on_scalar):
+            load, t0, width, cut = PIECES[i]
+            lo, hi = (0, cut) if on_scalar else (cut, width)
+            if lo == hi:
+                return
+            base = t0 - LOADS[load][1]
+            dst = xb[i][:, lo:hi, :].rearrange("p (c i) j -> p c j i", i=4)
+            src = xf[load][:, :, base + lo : base + hi].rearrange("p j (c i) -> p c j i", i=4)
+            if on_scalar:
+                nc.scalar.activation(dst, src, COPY)
+            else:
+                nc.vector.tensor_copy(out=dst, in_=src)
+
+        def quantise(i):
+            load, t0, width, _ = PIECES[i]
+            s = LOADS[load][0]
+            nc.vector.quantize_mx(
+                out=words[s][:, t0 : t0 + width].bitcast(E4M3),
+                scales=scales[s][:, t0 : t0 + width],
+                in_=xb[i][:].rearrange("p t j -> p (t j)"),
+            )
+
+        def pick(s, slots):
+            lst = offsets[:, slots.start // 16 : slots.stop // 16]
+            nc.vector.tensor_copy(gw[s][:, slots], words[s][:].indirect(lst))
+            nc.vector.tensor_copy(gs[s][:, slots], scales[s][:].indirect(lst))
+
+        def first(s, u):
+            e = u // (C // P)
+            cols = slice(u * P, (u + 1) * P)
+            nc.tensor.matmul_mx(
+                out=acc[u][:],
+                lhsT=gw[s][:, cols].bitcast(E4M3),
+                lhsT_scale=gs[s][:, cols],
+                rhs=w1[:, e, s, :].bitcast(E2M1),
+                rhs_scale=w1s[:, e, s * H : (s + 1) * H],
+                start=(s == 0),
+                stop=(s == PASSES - 1),
+            )
+
+        last = PASSES - 1
+        for s in range(PASSES):
+            mine = [i for i, x in enumerate(PIECES) if LOADS[x[0]][0] == s]
+            for i in mine:
+                cast(i, True)
+            if s > 0:
+                pick(s - 1, slice(0, S) if s < last else slice(0, C))
+                if s == last:
+                    first(0, 2)
+                    first(0, 3)
+                first(s - 1, 0)
+                first(s - 1, 1)
+            cast(mine[0], False)
+            for i in mine[1:]:
+                cast(i, False)
+                quantise(i - 1)
+            quantise(mine[-1])
+        pick(last, groups[0])
+        pick(last, groups[1])
+        pick(last - 1, groups[2])
+        pick(last, groups[2])
+        first(1, 2)
+        first(1, 3)
+
+        def turn(g, v, u, turned):
+            pairs = h[u][:].bitcast(F32)
+            for w in range(2):
+                nc.tensor.transpose(turned[:, v, w, :], pairs[:, w : 2 * P : 2], ident[:])
+
+        def weave(g, v, turned):
+            dst = hg[g][:, v * P : (v + 1) * P, :].rearrange("p r j -> p (r j)").bitcast(F32)
+            nc.scalar.copy(out=dst.rearrange("p (r w) -> p r w", w=2), in_=turned[:, v, :, :].rearrange("p w r -> p r w"))
+
+        def activate(u):
+            nc.scalar.activation(h[u][:], acc[u][:], RELU)
+
+        def quantise_h(g):
+            nc.vector.quantize_mx(
+                out=hq[g][:].bitcast(E4M3), scales=hs[g][:], in_=hg[g][:].rearrange("p r j -> p (r j)")
+            )
+
+        def second(g, e, outs):
+            for n in range(N_TILES):
+                nc.tensor.matmul_mx(
+                    out=outs[n],
+                    lhsT=w2[:, e, 2 * P * n : 2 * P * (n + 1)].bitcast(E2M1),
+                    lhsT_scale=w2s[:, e, n * P : (n + 1) * P],
+                    rhs=hq[g][:].bitcast(E4M3),
+                    rhs_scale=hs[g][:],
+                    start=True,
+                    stop=True,
+                )
+
+        def scatter(g, n, ready):
+            lst = offsets[:, groups[g].start // 16 : groups[g].stop // 16]
+            if ready:
+                nc.vector.tensor_copy(back[n][:].indirect(lst), ys[g][:, n, :])
+            else:
+                nc.vector.tensor_tensor(back[n][:].indirect(lst), yv[g][:, n, :], gates[:, groups[g]], MULT)
+
+        def add(engine, n, cols):
+            engine.tensor_tensor(res[n][:, cols], back[n][:, cols], res[n][:, cols], ADD)
+            nc.sync.dma_start(out=out[n * P : (n + 1) * P, cols], in_=res[n][:, cols])
+
+        turned0 = psum.tile([P, 1, 2, P], F32, name="turned0", tag="turned", bufs=2)
+        turned1 = psum.tile([P, 1, 2, P], F32, name="turned1", tag="turned", bufs=2)
+        first(last, 0)
+        first(last, 1)
+        first(2, 2)
+        first(2, 3)
+        activate(0)
+        activate(1)
+        turn(0, 0, 0, turned0)
+        first(last, 2)
+        first(last, 3)
+        weave(0, 0, turned0)
+        quantise_h(0)
+        y0 = psum.tile([P, N_TILES, P], F32, name="y0", tag="y", bufs=2)
+        second(0, 0, [y0[:, n, :] for n in range(N_TILES)])
+        turn(1, 0, 1, turned1)
+        activate(2)
+        nc.scalar.copy(out=yv[0][:], in_=y0[:])
+        activate(3)
+        weave(1, 0, turned1)
+        turned2 = psum.tile([P, 2, 2, P], F32, name="turned2", tag="turned", bufs=2)
+        turn(2, 0, 2, turned2)
+        turn(2, 1, 3, turned2)
+        weave(2, 0, turned2)
+        weave(2, 1, turned2)
+        scatter(0, 0, False)
+        quantise_h(1)
+        y1 = psum.tile([P, N_TILES, P], F32, name="y1", tag="y", bufs=2)
+        second(1, 0, [y1[:, n, :] for n in range(N_TILES)])
+        nc.scalar.copy(out=yv[1][:], in_=y1[:])
+        quantise_h(2)
+        y2a = psum.tile([P, 2, C], F32, name="y2a", tag="acc", bufs=U_TILES)
+        y2b = psum.tile([P, C], F32, name="y2b", tag="acc", bufs=U_TILES)
+        second(2, 1, [y2a[:, 0, :], y2a[:, 1, :], y2b[:]])
+        nc.scalar.copy(out=yv[2][:, 0:2, :], in_=y2a[:])
+        nc.scalar.copy(out=yv[2][:, 2, :], in_=y2b[:])
+        for n in (1, 2):
+            nc.gpsimd.tensor_tensor(ys[2][:, n, :], yv[2][:, n, :], gates[:, groups[2]], MULT)
+        scatter(0, 1, False)
+        scatter(0, 2, False)
+        for n in range(N_TILES):
+            scatter(1, n, False)
+        scatter(2, 0, False)
+        add(nc.gpsimd, 0, slice(0, T))
+        scatter(2, 1, True)
+        add(nc.gpsimd, 1, slice(0, 768))
+        scatter(2, 2, True)
+        add(nc.vector, 1, slice(768, T))
+        add(nc.vector, 2, slice(0, 512))
+        add(nc.vector, 2, slice(512, T))

@@ -8,11 +8,11 @@ P = 128
 PACK = 4
 PASSES = K // (P * PACK)
 S = E * C
-U_TILES = S // P
+GROUPS = S // P
 N_TILES = N // P
 
 FLOPS = 2 * S * (K * H + H * N)
-BYTES = 4 * (K * T + 2 * N * T + P * S) + E * (K * H + H * N) // 2 + E * (K * H + H * N) // 32 + 2 * P * S // 16
+BYTES = 4 * (K * T + 2 * N * T + S) + E * (K * H + H * N) // 2 + E * (K * H + H * N) // 32 + 2 * P * S // 16
 
 F32 = mybir.dt.float32
 BF16 = mybir.dt.bfloat16
@@ -27,9 +27,12 @@ RELU = mybir.ActivationFunctionType.Relu
 MULT = mybir.AluOpType.mult
 ADD = mybir.AluOpType.add
 
-LOADS = [(0, 0, 1024), (1, 0, 1024), (2, 0, 1024), (3, 0, 512), (3, 512, 256), (3, 768, 256)]
-PIECES = [(0, 0, 512, 0), (0, 512, 512, 512), (1, 0, 512, 304), (1, 512, 512, 304), (2, 0, 512, 256), (2, 512, 512, 304)] + [
-    (3, 0, 512, 416), (4, 512, 256, 200), (5, 768, 256, 120)]
+PIECES = [
+    (0, 0, 512, 176), (0, 512, 512, 176),
+    (1, 0, 512, 512), (1, 512, 512, 304),
+    (2, 0, 512, 512), (2, 512, 512, 304),
+    (3, 0, 512, 416), (3, 512, 256, 176), (3, 768, 256, 112),
+]
 
 
 def tile_moe_res_mlp_relu_kernel(
@@ -38,240 +41,266 @@ def tile_moe_res_mlp_relu_kernel(
     nc = tc.nc
     with ExitStack() as ctx:
         keep = ctx.enter_context(tc.tile_pool(name="keep", bufs=1))
+        turns = ctx.enter_context(tc.tile_pool(name="turns", bufs=1))
         psum = ctx.enter_context(tc.psum_pool(name="psum", bufs=1))
 
-        groups = (slice(0, P), slice(P, 2 * P), slice(C, S))
-        sizes = [g.stop - g.start for g in groups]
-        offsets = keep.tile([P, S // 16], U16, name="offsets")
-        w1s = keep.tile([P, E, PASSES * H], U8, name="w1s", align_bytes=64)
-        w2s = keep.tile([P, E, N], U8, name="w2s", align_bytes=64)
-        w1 = keep.tile([P, E, PASSES, 2 * H], U8, name="w1", align_bytes=64)
-        w2 = keep.tile([P, E, 2 * N], U8, name="w2", align_bytes=64)
-        gates = keep.tile([P, S], F32, name="gates")
-        warm = keep.tile([P, 8], F32, name="warm")
-        ident = keep.tile([P, P], F32, name="ident", align_bytes=64)
-        xf = [keep.tile([P, PACK, x[2]], F32, name=f"xf{i}", align_bytes=64) for i, x in enumerate(LOADS)]
-        xb = [keep.tile([P, x[2], PACK], BF16, name=f"xb{i}", align_bytes=64) for i, x in enumerate(PIECES)]
-        words = [keep.tile([P, T], U32, name=f"words{s}", align_bytes=64) for s in range(PASSES)]
-        scales = [keep.tile([P, T], U8, name=f"scales{s}", align_bytes=64) for s in range(PASSES)]
-        gw = [keep.tile([P, S], U32, name=f"gw{s}", align_bytes=64) for s in range(PASSES)]
-        gs = [keep.tile([P, S], U8, name=f"gs{s}", align_bytes=64) for s in range(PASSES)]
-        h = [keep.tile([P, H], BF16, name=f"h{u}", align_bytes=64) for u in range(U_TILES)]
-        hg = [keep.tile([P, n, PACK], BF16, name=f"hg{g}", align_bytes=64) for g, n in enumerate(sizes)]
-        hq = [keep.tile([P, n], U32, name=f"hq{g}", align_bytes=64) for g, n in enumerate(sizes)]
-        hs = [keep.tile([P, n], U8, name=f"hs{g}", align_bytes=64) for g, n in enumerate(sizes)]
-        yv = [keep.tile([P, N_TILES, n], F32, name=f"yv{g}", align_bytes=64) for g, n in enumerate(sizes)]
-        ys = [keep.tile([P, N_TILES, n], F32, name=f"ys{g}", align_bytes=64) for g, n in enumerate(sizes)]
-        back = [keep.tile([P, T], F32, name=f"back{n}", align_bytes=64) for n in range(N_TILES)]
-        res = [keep.tile([P, T], F32, name=f"res{n}", align_bytes=64) for n in range(N_TILES)]
+        def sb(shape, dtype, name):
+            return keep.tile(shape, dtype, name=name, align_bytes=64)
 
+        def bank(b, shape, name):
+            return psum.tile(shape, F32, name=name, tag=f"bank{b}", bufs=1)
+
+        offsets = keep.tile([P, S // 16], U16, name="offsets")
+        w1s = sb([P, E, PASSES * H], U8, "w1s")
+        w2s = sb([P, E, N], U8, "w2s")
+        w1 = [[sb([P, 2, 2 * H], U8, f"w1_{e}_{a}") for a in range(2)] for e in range(E)]
+        w2 = sb([P, E, 2 * N], U8, "w2")
+        gate_rows = sb([P, P], F32, "gate_rows")
+        gate_cols = sb([P, GROUPS], F32, "gate_cols")
+        gates = sb([P, S], F32, "gates")
+        warm = sb([P, 8], F32, "warm")
+        ident = sb([P, P], F32, "ident")
+        xf = [sb([P, PACK, x[2]], F32, f"xf{i}") for i, x in enumerate(PIECES)]
+        xb = [sb([P, x[2], PACK], BF16, f"xb{i}") for i, x in enumerate(PIECES[:-1])]
+        xb.append(turns.tile([P, PIECES[-1][2], PACK], BF16, name="xb_last", align_bytes=64, offset=0))
+        words = [sb([P, T], U32, f"words{s}") for s in range(PASSES)]
+        scales = [sb([P, T], U8, f"scales{s}") for s in range(PASSES)]
+        picked = {}
+        h = [sb([P, H], BF16, f"h{g}") for g in range(GROUPS)]
+        hg = [turns.tile([P, P, PACK], BF16, name="hg0", align_bytes=64, offset=2048)]
+        hg.extend(sb([P, P, PACK], BF16, f"hg{g}") for g in range(1, GROUPS))
+        hq = [sb([P, P], U32, f"hq{g}") for g in range(GROUPS)]
+        hs = [sb([P, P], U8, f"hs{g}") for g in range(GROUPS)]
+        y_first = [sb([P, P], F32, f"y_first{g}") for g in range(GROUPS)]
+        y_rest0 = sb([P, 2, P], F32, "y_rest0")
+        y_slot = [sb([P, 2 * P], F32, f"y_slot{g}") for g in range(1, GROUPS)]
+        y_gated = [sb([P, S - P], F32, f"y_gated{n}") for n in range(1, N_TILES)]
+        back = [sb([P, T], F32, f"back{n}") for n in range(N_TILES)]
+        res = [sb([P, T], F32, f"res{n}") for n in range(N_TILES)]
+
+        nc.vector.memset(gate_rows[:], 0.0)
+        for s in range(PASSES):
+            nc.vector.memset(scales[s][:].bitcast(I32), 0)
         nc.vector.memset(w1s[:].rearrange("p e i -> p (e i)").bitcast(I32), 0)
         nc.vector.memset(w2s[:].rearrange("p e i -> p (e i)").bitcast(I32), 0)
         nc.vector.memset(warm[:], 0.0)
-        for n in range(N_TILES):
-            nc.vector.memset(back[n][:], 0.0)
-        for s in range(PASSES):
-            nc.gpsimd.memset(scales[s][:].bitcast(I32), 0)
+        nc.scalar.activation(warm[:], warm[:], RELU)
         make_identity(nc, ident[:])
-
-        nc.sync.dma_start(offsets[:], offs)
+        for n in range(N_TILES):
+            nc.gpsimd.memset(back[n][:], 0.0)
 
         def load_x(i):
-            s, t0, width = LOADS[i]
+            s, t0, width, _ = PIECES[i]
             rows = xT[s * P * PACK : (s + 1) * P * PACK, t0 : t0 + width]
             nc.sync.dma_start(out=xf[i][:], in_=rows.rearrange("(p j) t -> p j t", j=PACK))
 
-        def load_w1(e, s0):
+        def load_w1(e, a):
             nc.sync.dma_start(
-                out=w1[:, e, s0 : s0 + 2, :].bitcast(I32),
-                in_=w1_words[e, s0 : s0 + 2, :, :].bitcast(I32).rearrange("s p b -> p s b"),
+                out=w1[e][a][:].bitcast(I32),
+                in_=w1_words[e, 2 * a : 2 * a + 2, :, :].bitcast(I32).rearrange("s p b -> p s b"),
             )
 
-        def load_w1_scales(queue, e):
+        def load_w1_scales(e):
             rows = w1_scales[e].bitcast(I32)
-            for q in range(4):
-                queue.dma_start(
-                    out=w1s[32 * q : 32 * q + 4, e, :].bitcast(I32).rearrange("q (s i) -> q s i", s=PASSES),
-                    in_=rows[:, 4 * q : 4 * q + 4, :].rearrange("s q i -> q s i"),
+            for r in range(4):
+                nc.sync.dma_start(
+                    out=w1s[r:P:32, e, :].bitcast(I32).rearrange("q (s i) -> q s i", s=PASSES),
+                    in_=rows[:, r:16:4, :].rearrange("s q i -> q s i"),
                 )
 
-        load_w1_scales(nc.scalar, 0)
         load_x(0)
-        load_x(1)
+        nc.sync.dma_start(offsets[:], offs)
+        nc.sync.dma_start(out=gate_rows[0:GROUPS, :], in_=gate[0, :].rearrange("(g p) -> g p", p=P))
+        for i in range(1, 6):
+            load_x(i)
+        load_w1_scales(0)
+        load_x(6)
         load_w1(0, 0)
-        load_x(2)
-        load_w1(0, 2)
-        load_x(3)
-        load_x(4)
-        load_w1_scales(nc.sync, 1)
+        load_x(7)
+        load_x(8)
+        load_w1(0, 1)
+        load_w1_scales(1)
         load_w1(1, 0)
-        load_x(5)
-        nc.sync.dma_start(out=gates[:], in_=gate[0:P, :])
-        load_w1(1, 2)
+        load_w1(1, 1)
         nc.sync.dma_start(out=w2[:].bitcast(I32), in_=w2_words[:, 0, :, :].bitcast(I32).rearrange("e p b -> p e b"))
         rows = w2_scales[:, 0, :, :].bitcast(I32)
-        for q in range(4):
+        for r in range(4):
             nc.sync.dma_start(
-                out=w2s[32 * q : 32 * q + 4, :, :].bitcast(I32),
-                in_=rows[:, 4 * q : 4 * q + 4, :].rearrange("e q i -> q e i"),
+                out=w2s[r:P:32, :, :].bitcast(I32),
+                in_=rows[:, r:16:4, :].rearrange("e q i -> q e i"),
             )
         for n in range(N_TILES):
             nc.sync.dma_start(out=res[n][:], in_=xr[n * P : (n + 1) * P, :])
 
-        nc.scalar.activation(warm[:], warm[:], RELU)
-        acc = [psum.tile([P, H], F32, name=f"acc{u}", tag="acc", bufs=U_TILES) for u in range(U_TILES)]
+        turned_gate = bank(4, [P, P], "turned_gate")
+        nc.tensor.transpose(turned_gate[:], gate_rows[:], ident[:])
+        nc.scalar.copy(out=gate_cols[:], in_=turned_gate[:, 0:GROUPS])
+        spread_gate = bank(5, [P, GROUPS, P], "spread_gate")
+        for g in range(GROUPS):
+            nc.tensor.transpose(spread_gate[:, g, :], gate_cols[:, g : g + 1].to_broadcast([P, P]), ident[:])
+        nc.scalar.copy(out=gates[:], in_=spread_gate[:].rearrange("p g r -> p (g r)"))
+
+        acc = [bank(g, [P, H], f"acc{g}") for g in range(GROUPS)]
 
         def cast(i, on_scalar):
-            load, t0, width, cut = PIECES[i]
+            _, _, width, cut = PIECES[i]
             lo, hi = (0, cut) if on_scalar else (cut, width)
             if lo == hi:
                 return
-            base = t0 - LOADS[load][1]
             dst = xb[i][:, lo:hi, :].rearrange("p (c i) j -> p c j i", i=4)
-            src = xf[load][:, :, base + lo : base + hi].rearrange("p j (c i) -> p c j i", i=4)
+            src = xf[i][:, :, lo:hi].rearrange("p j (c i) -> p c j i", i=4)
             if on_scalar:
                 nc.scalar.activation(dst, src, COPY)
             else:
                 nc.vector.tensor_copy(out=dst, in_=src)
 
         def quantise(i):
-            load, t0, width, _ = PIECES[i]
-            s = LOADS[load][0]
+            s, t0, width, _ = PIECES[i]
             nc.vector.quantize_mx(
                 out=words[s][:, t0 : t0 + width].bitcast(E4M3),
                 scales=scales[s][:, t0 : t0 + width],
                 in_=xb[i][:].rearrange("p t j -> p (t j)"),
             )
 
-        def pick(s, slots):
-            lst = offsets[:, slots.start // 16 : slots.stop // 16]
-            nc.vector.tensor_copy(gw[s][:, slots], words[s][:].indirect(lst))
-            nc.vector.tensor_copy(gs[s][:, slots], scales[s][:].indirect(lst))
+        def listed(lo, hi):
+            return offsets[:, lo // 16 : hi // 16]
 
-        def first(s, u):
-            e = u // (C // P)
-            cols = slice(u * P, (u + 1) * P)
+        def pick(s, lo, hi, offset=None):
+            n = hi - lo
+            if offset is None:
+                gw, gs = sb([P, n], U32, f"gw{s}_{lo}"), sb([P, n], U8, f"gs{s}_{lo}")
+            else:
+                gw = turns.tile([P, n], U32, name=f"gw{s}_{lo}", align_bytes=64, offset=offset)
+                gs = turns.tile([P, n], U8, name=f"gs{s}_{lo}", align_bytes=64, offset=offset + 4 * n)
+            nc.vector.tensor_copy(gw[:], words[s][:].indirect(listed(lo, hi)))
+            nc.vector.tensor_copy(gs[:], scales[s][:].indirect(listed(lo, hi)))
+            for g in range(lo // P, hi // P):
+                cols = slice(g * P - lo, (g + 1) * P - lo)
+                picked[s, g] = (gw[:, cols], gs[:, cols])
+
+        def first(s, g):
+            e = g // (C // P)
             nc.tensor.matmul_mx(
-                out=acc[u][:],
-                lhsT=gw[s][:, cols].bitcast(E4M3),
-                lhsT_scale=gs[s][:, cols],
-                rhs=w1[:, e, s, :].bitcast(E2M1),
+                out=acc[g][:],
+                lhsT=picked[s, g][0].bitcast(E4M3),
+                lhsT_scale=picked[s, g][1],
+                rhs=w1[e][s // 2][:, s % 2, :].bitcast(E2M1),
                 rhs_scale=w1s[:, e, s * H : (s + 1) * H],
                 start=(s == 0),
                 stop=(s == PASSES - 1),
             )
 
         last = PASSES - 1
-        for s in range(PASSES):
-            mine = [i for i, x in enumerate(PIECES) if LOADS[x[0]][0] == s]
-            for i in mine:
-                cast(i, True)
-            if s > 0:
-                pick(s - 1, slice(0, S) if s < last else slice(0, C))
-                if s == last:
-                    first(0, 2)
-                    first(0, 3)
-                first(s - 1, 0)
-                first(s - 1, 1)
-            cast(mine[0], False)
-            for i in mine[1:]:
-                cast(i, False)
-                quantise(i - 1)
-            quantise(mine[-1])
-        pick(last, groups[0])
-        pick(last, groups[1])
-        pick(last - 1, groups[2])
-        pick(last, groups[2])
-        first(1, 2)
-        first(1, 3)
+        for i, x in enumerate(PIECES):
+            cast(i, True)
+            cast(i, False)
+            quantise(i)
+            if x[1] + x[2] == T and x[0] < last:
+                pick(x[0], 0, S if x[0] < last - 1 else C)
+        pick(last, 0, P)
+        pick(last, P, C)
+        pick(last - 1, C, S, 0)
+        pick(last, C, C + P)
 
-        def turn(g, v, u, turned):
-            pairs = h[u][:].bitcast(F32)
+        def activate(g):
+            nc.scalar.activation(
+                h[g][:].rearrange("p (w r e) -> p w r e", w=2, e=2),
+                acc[g][:].rearrange("p (r w e) -> p w r e", w=2, e=2),
+                RELU,
+            )
+
+        def turn(g, b):
+            turned = bank(b, [P, 2, P], f"turned{g}")
+            pairs = h[g][:].bitcast(F32)
             for w in range(2):
-                nc.tensor.transpose(turned[:, v, w, :], pairs[:, w : 2 * P : 2], ident[:])
-
-        def weave(g, v, turned):
-            dst = hg[g][:, v * P : (v + 1) * P, :].rearrange("p r j -> p (r j)").bitcast(F32)
-            nc.scalar.copy(out=dst.rearrange("p (r w) -> p r w", w=2), in_=turned[:, v, :, :].rearrange("p w r -> p r w"))
-
-        def activate(u):
-            nc.scalar.activation(h[u][:], acc[u][:], RELU)
-
-        def quantise_h(g):
+                nc.tensor.transpose(turned[:, w, :], pairs[:, w * P : (w + 1) * P], ident[:])
+            dst = hg[g][:].rearrange("p r j -> p (r j)").bitcast(F32)
+            nc.scalar.copy(out=dst.rearrange("p (r w) -> p r w", w=2), in_=turned[:].rearrange("p w r -> p r w"))
             nc.vector.quantize_mx(
                 out=hq[g][:].bitcast(E4M3), scales=hs[g][:], in_=hg[g][:].rearrange("p r j -> p (r j)")
             )
 
-        def second(g, e, outs):
-            for n in range(N_TILES):
-                nc.tensor.matmul_mx(
-                    out=outs[n],
-                    lhsT=w2[:, e, 2 * P * n : 2 * P * (n + 1)].bitcast(E2M1),
-                    lhsT_scale=w2s[:, e, n * P : (n + 1) * P],
-                    rhs=hq[g][:].bitcast(E4M3),
-                    rhs_scale=hs[g][:],
-                    start=True,
-                    stop=True,
-                )
+        def second(g, n, dst):
+            e = g // (C // P)
+            nc.tensor.matmul_mx(
+                out=dst,
+                lhsT=w2[:, e, 2 * P * n : 2 * P * (n + 1)].bitcast(E2M1),
+                lhsT_scale=w2s[:, e, n * P : (n + 1) * P],
+                rhs=hq[g][:].bitcast(E4M3),
+                rhs_scale=hs[g][:],
+                start=True,
+                stop=True,
+            )
 
-        def scatter(g, n, ready):
-            lst = offsets[:, groups[g].start // 16 : groups[g].stop // 16]
-            if ready:
-                nc.vector.tensor_copy(back[n][:].indirect(lst), ys[g][:, n, :])
-            else:
-                nc.vector.tensor_tensor(back[n][:].indirect(lst), yv[g][:, n, :], gates[:, groups[g]], MULT)
+        def first_rows(g, b):
+            y = bank(b, [P, P], f"y{g}")
+            second(g, 0, y[:])
+            nc.scalar.copy(out=y_first[g][:], in_=y[:])
+            lo, hi = g * P, (g + 1) * P
+            nc.vector.tensor_tensor(back[0][:].indirect(listed(lo, hi)), y_first[g][:], gates[:, lo:hi], MULT)
 
-        def add(engine, n, cols):
-            engine.tensor_tensor(res[n][:, cols], back[n][:, cols], res[n][:, cols], ADD)
-            nc.sync.dma_start(out=out[n * P : (n + 1) * P, cols], in_=res[n][:, cols])
+        def rest_rows_group0(b):
+            y = bank(b, [P, 2, P], "y0_rest")
+            for n in (1, 2):
+                second(0, n, y[:, n - 1, :])
+            nc.scalar.copy(out=y_rest0[:], in_=y[:])
+            for n in (1, 2):
+                nc.vector.tensor_tensor(back[n][:].indirect(listed(0, P)), y_rest0[:, n - 1, :], gates[:, 0:P], MULT)
 
-        turned0 = psum.tile([P, 1, 2, P], F32, name="turned0", tag="turned", bufs=2)
-        turned1 = psum.tile([P, 1, 2, P], F32, name="turned1", tag="turned", bufs=2)
+        def rest_by_slot(g):
+            e = g // (C // P)
+            y = bank(g, [P, 2 * P], f"y_slot{g}")
+            nc.tensor.matmul_mx(
+                out=y[:],
+                lhsT=hq[g][:].bitcast(E4M3),
+                lhsT_scale=hs[g][:],
+                rhs=w2[:, e, 2 * P : 2 * N].bitcast(E2M1),
+                rhs_scale=w2s[:, e, P:N],
+                start=True,
+                stop=True,
+            )
+            nc.scalar.activation(y_slot[g - 1][:], y[:], COPY, scale=gate_cols[:, g : g + 1])
+
+        def rest_rows(n, b):
+            y = bank(b, [P, GROUPS - 1, P], f"y_back{n}")
+            for g in range(1, GROUPS):
+                nc.tensor.transpose(y[:, g - 1, :], y_slot[g - 1][:, (n - 1) * P : n * P], ident[:])
+            nc.scalar.copy(out=y_gated[n - 1][:], in_=y[:].rearrange("p g r -> p (g r)"))
+            nc.vector.tensor_copy(back[n][:].indirect(listed(P, S)), y_gated[n - 1][:])
+
+        def add(engine, n, lo, hi):
+            engine.tensor_tensor(res[n][:, lo:hi], back[n][:, lo:hi], res[n][:, lo:hi], ADD)
+            nc.sync.dma_start(out=out[n * P : (n + 1) * P, lo:hi], in_=res[n][:, lo:hi])
+
+        for g in (0, 1):
+            for s in range(last):
+                first(s, g)
         first(last, 0)
-        first(last, 1)
-        first(2, 2)
-        first(2, 3)
         activate(0)
+        turn(0, 4)
+        pick(last, C + P, S, 2048)
+        first_rows(0, 5)
+        first(last, 1)
         activate(1)
-        turn(0, 0, 0, turned0)
-        first(last, 2)
-        first(last, 3)
-        weave(0, 0, turned0)
-        quantise_h(0)
-        y0 = psum.tile([P, N_TILES, P], F32, name="y0", tag="y", bufs=2)
-        second(0, 0, [y0[:, n, :] for n in range(N_TILES)])
-        turn(1, 0, 1, turned1)
+        turn(1, 6)
+        rest_rows_group0(6)
+        for s in range(PASSES):
+            first(s, 2)
         activate(2)
-        nc.scalar.copy(out=yv[0][:], in_=y0[:])
+        turn(2, 4)
+        first_rows(1, 4)
+        for s in range(PASSES):
+            first(s, 3)
         activate(3)
-        weave(1, 0, turned1)
-        turned2 = psum.tile([P, 2, 2, P], F32, name="turned2", tag="turned", bufs=2)
-        turn(2, 0, 2, turned2)
-        turn(2, 1, 3, turned2)
-        weave(2, 0, turned2)
-        weave(2, 1, turned2)
-        scatter(0, 0, False)
-        quantise_h(1)
-        y1 = psum.tile([P, N_TILES, P], F32, name="y1", tag="y", bufs=2)
-        second(1, 0, [y1[:, n, :] for n in range(N_TILES)])
-        nc.scalar.copy(out=yv[1][:], in_=y1[:])
-        quantise_h(2)
-        y2a = psum.tile([P, 2, C], F32, name="y2a", tag="acc", bufs=U_TILES)
-        y2b = psum.tile([P, C], F32, name="y2b", tag="acc", bufs=U_TILES)
-        second(2, 1, [y2a[:, 0, :], y2a[:, 1, :], y2b[:]])
-        nc.scalar.copy(out=yv[2][:, 0:2, :], in_=y2a[:])
-        nc.scalar.copy(out=yv[2][:, 2, :], in_=y2b[:])
-        for n in (1, 2):
-            nc.gpsimd.tensor_tensor(ys[2][:, n, :], yv[2][:, n, :], gates[:, groups[2]], MULT)
-        scatter(0, 1, False)
-        scatter(0, 2, False)
-        for n in range(N_TILES):
-            scatter(1, n, False)
-        scatter(2, 0, False)
-        add(nc.gpsimd, 0, slice(0, T))
-        scatter(2, 1, True)
-        add(nc.gpsimd, 1, slice(0, 768))
-        scatter(2, 2, True)
-        add(nc.vector, 1, slice(768, T))
-        add(nc.vector, 2, slice(0, 512))
-        add(nc.vector, 2, slice(512, T))
+        turn(3, 7)
+        first_rows(2, 7)
+        first_rows(3, 5)
+        for g in range(1, GROUPS):
+            rest_by_slot(g)
+        add(nc.gpsimd, 0, 0, T)
+        rest_rows(1, 0)
+        add(nc.gpsimd, 1, 0, 512)
+        add(nc.gpsimd, 1, 512, T)
+        rest_rows(2, 6)
+        for lo in range(0, T, 256):
+            add(nc.vector, 2, lo, lo + 256)

@@ -27,11 +27,13 @@ RELU = mybir.ActivationFunctionType.Relu
 MULT = mybir.AluOpType.mult
 ADD = mybir.AluOpType.add
 
-PIECES = [
-    (0, 0, 512, 176), (0, 512, 512, 176),
-    (1, 0, 512, 512), (1, 512, 512, 304),
-    (2, 0, 512, 512), (2, 512, 512, 304),
-    (3, 0, 512, 416), (3, 512, 256, 176), (3, 768, 256, 112),
+LOADS = [(0, 0, 512), (0, 512, T), (1, 0, 512), (1, 512, T), (2, 0, 512), (2, 512, T), (3, 0, 512), (3, 512, 896), (3, 896, T)]
+PIECES = [(0, 0, 512), (0, 512, T), (1, 0, 512), (1, 512, T), (2, 0, 512), (2, 512, T), (3, 0, 256), (3, 256, 512), (3, 512, 768), (3, 768, T)]
+CASTS = [
+    (0, 0, 176, 512), (0, 512, 688, T),
+    (1, 0, 512, 512), (1, 512, 768, T),
+    (2, 0, 512, 512), (2, 512, 768, T),
+    (3, 0, 256, 256), (3, 256, 384, 512), (3, 512, 768, 768), (3, 768, 768, 896), (3, 896, 952, T),
 ]
 
 
@@ -47,6 +49,9 @@ def tile_moe_res_mlp_relu_kernel(
         def sb(shape, dtype, name):
             return keep.tile(shape, dtype, name=name, align_bytes=64)
 
+        def at(offset, shape, dtype, name):
+            return turns.tile(shape, dtype, name=name, align_bytes=64, offset=offset)
+
         def bank(b, shape, name):
             return psum.tile(shape, F32, name=name, tag=f"bank{b}", bufs=1)
 
@@ -55,30 +60,28 @@ def tile_moe_res_mlp_relu_kernel(
         w2s = sb([P, E, N], U8, "w2s")
         w1 = [[sb([P, 2, 2 * H], U8, f"w1_{e}_{a}") for a in range(2)] for e in range(E)]
         w2 = sb([P, E, 2 * N], U8, "w2")
-        gate_rows = sb([P, P], F32, "gate_rows")
-        gate_cols = sb([P, GROUPS], F32, "gate_cols")
+        gate_four = sb([P, 4], F32, "gate_four")
+        gate_cols = sb([P, GROUPS - 1], F32, "gate_cols")
         gates = sb([P, S], F32, "gates")
         warm = sb([P, 8], F32, "warm")
         ident = sb([P, P], F32, "ident")
-        xf = [sb([P, PACK, x[2]], F32, f"xf{i}") for i, x in enumerate(PIECES)]
-        xb = [sb([P, x[2], PACK], BF16, f"xb{i}") for i, x in enumerate(PIECES[:-1])]
-        xb.append(turns.tile([P, PIECES[-1][2], PACK], BF16, name="xb_last", align_bytes=64, offset=0))
+        xf = [sb([P, PACK, x[2] - x[1]], F32, f"xf{i}") for i, x in enumerate(LOADS)]
+        xb = [sb([P, x[2] - x[1], PACK], BF16, f"xb{i}") for i, x in enumerate(PIECES[:-1])]
+        xb.append(turns.tile([P, PIECES[-1][2] - PIECES[-1][1], PACK], BF16, name="xb_last", align_bytes=64, offset=0))
         words = [sb([P, T], U32, f"words{s}") for s in range(PASSES)]
         scales = [sb([P, T], U8, f"scales{s}") for s in range(PASSES)]
         picked = {}
-        h = [sb([P, H], BF16, f"h{g}") for g in range(GROUPS)]
+        h = {}
+        h0 = [sb([P, H // 2], BF16, "h0_0"), sb([P, H // 2], BF16, "h0_1")]
         hg = [turns.tile([P, P, PACK], BF16, name="hg0", align_bytes=64, offset=2048)]
         hg.extend(sb([P, P, PACK], BF16, f"hg{g}") for g in range(1, GROUPS))
         hq = [sb([P, P], U32, f"hq{g}") for g in range(GROUPS)]
         hs = [sb([P, P], U8, f"hs{g}") for g in range(GROUPS)]
-        y_first = [sb([P, P], F32, f"y_first{g}") for g in range(GROUPS)]
-        y_rest0 = sb([P, 2, P], F32, "y_rest0")
         y_slot = [sb([P, 2 * P], F32, f"y_slot{g}") for g in range(1, GROUPS)]
         y_gated = [sb([P, S - P], F32, f"y_gated{n}") for n in range(1, N_TILES)]
         back = [sb([P, T], F32, f"back{n}") for n in range(N_TILES)]
         res = [sb([P, T], F32, f"res{n}") for n in range(N_TILES)]
 
-        nc.vector.memset(gate_rows[:], 0.0)
         for s in range(PASSES):
             nc.vector.memset(scales[s][:].bitcast(I32), 0)
         nc.vector.memset(w1s[:].rearrange("p e i -> p (e i)").bitcast(I32), 0)
@@ -90,8 +93,8 @@ def tile_moe_res_mlp_relu_kernel(
             nc.gpsimd.memset(back[n][:], 0.0)
 
         def load_x(i):
-            s, t0, width, _ = PIECES[i]
-            rows = xT[s * P * PACK : (s + 1) * P * PACK, t0 : t0 + width]
+            s, t0, t1 = LOADS[i]
+            rows = xT[s * P * PACK : (s + 1) * P * PACK, t0:t1]
             nc.sync.dma_start(out=xf[i][:], in_=rows.rearrange("(p j) t -> p j t", j=PACK))
 
         def load_w1(e, a):
@@ -100,26 +103,17 @@ def tile_moe_res_mlp_relu_kernel(
                 in_=w1_words[e, 2 * a : 2 * a + 2, :, :].bitcast(I32).rearrange("s p b -> p s b"),
             )
 
-        def load_w1_scales(e):
-            rows = w1_scales[e].bitcast(I32)
-            for r in range(4):
-                nc.sync.dma_start(
-                    out=w1s[r:P:32, e, :].bitcast(I32).rearrange("q (s i) -> q s i", s=PASSES),
-                    in_=rows[:, r:16:4, :].rearrange("s q i -> q s i"),
-                )
-
-        load_x(0)
+        nc.sync.dma_start(out=gate_four[:], in_=gate[0, :].rearrange("(p f) -> p f", f=4))
         nc.sync.dma_start(offsets[:], offs)
-        nc.sync.dma_start(out=gate_rows[0:GROUPS, :], in_=gate[0, :].rearrange("(g p) -> g p", p=P))
-        for i in range(1, 6):
+        for i in range(len(LOADS)):
             load_x(i)
-        load_w1_scales(0)
-        load_x(6)
+        rows = w1_scales.bitcast(I32).rearrange("e s q i -> q (e s) i")
+        for r in range(4):
+            nc.sync.dma_start(
+                out=w1s[r:P:32, :, :].bitcast(I32).rearrange("q e (s i) -> q (e s) i", s=PASSES), in_=rows[r:16:4, :, :]
+            )
         load_w1(0, 0)
-        load_x(7)
-        load_x(8)
         load_w1(0, 1)
-        load_w1_scales(1)
         load_w1(1, 0)
         load_w1(1, 1)
         nc.sync.dma_start(out=w2[:].bitcast(I32), in_=w2_words[:, 0, :, :].bitcast(I32).rearrange("e p b -> p e b"))
@@ -132,33 +126,36 @@ def tile_moe_res_mlp_relu_kernel(
         for n in range(N_TILES):
             nc.sync.dma_start(out=res[n][:], in_=xr[n * P : (n + 1) * P, :])
 
-        turned_gate = bank(4, [P, P], "turned_gate")
-        nc.tensor.transpose(turned_gate[:], gate_rows[:], ident[:])
-        nc.scalar.copy(out=gate_cols[:], in_=turned_gate[:, 0:GROUPS])
-        spread_gate = bank(5, [P, GROUPS, P], "spread_gate")
-        for g in range(GROUPS):
-            nc.tensor.transpose(spread_gate[:, g, :], gate_cols[:, g : g + 1].to_broadcast([P, P]), ident[:])
-        nc.scalar.copy(out=gates[:], in_=spread_gate[:].rearrange("p g r -> p (g r)"))
+        spread_gate = bank(4, [P, 4, P], "spread_gate")
+        for f in range(4):
+            nc.tensor.transpose(spread_gate[:, f, :], gate_four[:, f : f + 1].to_broadcast([P, P]), ident[:])
+        nc.scalar.copy(out=gates[:].rearrange("q (p f) -> q p f", f=4), in_=spread_gate[:].rearrange("q f p -> q p f"))
+        turned_gate = bank(5, [P, GROUPS - 1, P], "turned_gate")
+        for g in range(1, GROUPS):
+            nc.tensor.transpose(turned_gate[:, g - 1, :], gates[:, g * P : (g + 1) * P], ident[:])
+        nc.scalar.copy(out=gate_cols[:], in_=turned_gate[:, :, 0])
 
         acc = [bank(g, [P, H], f"acc{g}") for g in range(GROUPS)]
 
-        def cast(i, on_scalar):
-            _, _, width, cut = PIECES[i]
-            lo, hi = (0, cut) if on_scalar else (cut, width)
+        def holder(parts, s, t):
+            return [i for i, x in enumerate(parts) if x[0] == s and x[1] <= t < x[2]][0]
+
+        def cast(s, lo, hi, on_scalar):
             if lo == hi:
                 return
-            dst = xb[i][:, lo:hi, :].rearrange("p (c i) j -> p c j i", i=4)
-            src = xf[i][:, :, lo:hi].rearrange("p j (c i) -> p c j i", i=4)
+            a, b = holder(LOADS, s, lo), holder(PIECES, s, lo)
+            dst = xb[b][:, lo - PIECES[b][1] : hi - PIECES[b][1], :].rearrange("p (c i) j -> p c j i", i=4)
+            src = xf[a][:, :, lo - LOADS[a][1] : hi - LOADS[a][1]].rearrange("p j (c i) -> p c j i", i=4)
             if on_scalar:
                 nc.scalar.activation(dst, src, COPY)
             else:
                 nc.vector.tensor_copy(out=dst, in_=src)
 
         def quantise(i):
-            s, t0, width, _ = PIECES[i]
+            s, t0, t1 = PIECES[i]
             nc.vector.quantize_mx(
-                out=words[s][:, t0 : t0 + width].bitcast(E4M3),
-                scales=scales[s][:, t0 : t0 + width],
+                out=words[s][:, t0:t1].bitcast(E4M3),
+                scales=scales[s][:, t0:t1],
                 in_=xb[i][:].rearrange("p t j -> p (t j)"),
             )
 
@@ -191,18 +188,28 @@ def tile_moe_res_mlp_relu_kernel(
             )
 
         last = PASSES - 1
-        for i, x in enumerate(PIECES):
-            cast(i, True)
-            cast(i, False)
-            quantise(i)
-            if x[1] + x[2] == T and x[0] < last:
-                pick(x[0], 0, S if x[0] < last - 1 else C)
+        done = {}
+        for s, lo, cut, hi in CASTS:
+            cast(s, lo, cut, True)
+            cast(s, cut, hi, False)
+            i = holder(PIECES, s, lo)
+            if PIECES[i][2] == hi:
+                quantise(i)
+            done[s] = done.get(s, 0) + hi - lo
+            if done[s] == T and s < last:
+                pick(s, 0, S if s < last - 1 else C)
         pick(last, 0, P)
         pick(last, P, C)
         pick(last - 1, C, S, 0)
         pick(last, C, C + P)
 
         def activate(g):
+            if g == 0:
+                for w in range(2):
+                    sums = acc[0][:].rearrange("p (r w e) -> p w r e", w=2, e=2)[:, w, :, :]
+                    nc.scalar.activation(h0[w][:].rearrange("p (r e) -> p r e", e=2), sums, RELU)
+                return
+            h[g] = sb([P, H], BF16, f"h{g}")
             nc.scalar.activation(
                 h[g][:].rearrange("p (w r e) -> p w r e", w=2, e=2),
                 acc[g][:].rearrange("p (r w e) -> p w r e", w=2, e=2),
@@ -211,9 +218,9 @@ def tile_moe_res_mlp_relu_kernel(
 
         def turn(g, b):
             turned = bank(b, [P, 2, P], f"turned{g}")
-            pairs = h[g][:].bitcast(F32)
             for w in range(2):
-                nc.tensor.transpose(turned[:, w, :], pairs[:, w * P : (w + 1) * P], ident[:])
+                pairs = h0[w][:].bitcast(F32) if g == 0 else h[g][:].bitcast(F32)[:, w * P : (w + 1) * P]
+                nc.tensor.transpose(turned[:, w, :], pairs, ident[:])
             dst = hg[g][:].rearrange("p r j -> p (r j)").bitcast(F32)
             nc.scalar.copy(out=dst.rearrange("p (r w) -> p r w", w=2), in_=turned[:].rearrange("p w r -> p r w"))
             nc.vector.quantize_mx(
@@ -235,21 +242,23 @@ def tile_moe_res_mlp_relu_kernel(
         def first_rows(g, b):
             y = bank(b, [P, P], f"y{g}")
             second(g, 0, y[:])
-            nc.scalar.copy(out=y_first[g][:], in_=y[:])
+            y_first = sb([P, P], F32, f"y_first{g}")
+            nc.scalar.copy(out=y_first[:], in_=y[:])
             lo, hi = g * P, (g + 1) * P
-            nc.vector.tensor_tensor(back[0][:].indirect(listed(lo, hi)), y_first[g][:], gates[:, lo:hi], MULT)
+            nc.vector.tensor_tensor(back[0][:].indirect(listed(lo, hi)), y_first[:], gates[:, lo:hi], MULT)
 
         def rest_rows_group0(b):
             y = bank(b, [P, 2, P], "y0_rest")
+            y_rest0 = sb([P, 2, P], F32, "y_rest0")
             for n in (1, 2):
                 second(0, n, y[:, n - 1, :])
             nc.scalar.copy(out=y_rest0[:], in_=y[:])
             for n in (1, 2):
                 nc.vector.tensor_tensor(back[n][:].indirect(listed(0, P)), y_rest0[:, n - 1, :], gates[:, 0:P], MULT)
 
-        def rest_by_slot(g):
+        def rest_by_slot(g, b):
             e = g // (C // P)
-            y = bank(g, [P, 2 * P], f"y_slot{g}")
+            y = bank(b, [P, 2 * P], f"y_slot{g}")
             nc.tensor.matmul_mx(
                 out=y[:],
                 lhsT=hq[g][:].bitcast(E4M3),
@@ -259,7 +268,7 @@ def tile_moe_res_mlp_relu_kernel(
                 start=True,
                 stop=True,
             )
-            nc.scalar.activation(y_slot[g - 1][:], y[:], COPY, scale=gate_cols[:, g : g + 1])
+            nc.scalar.activation(y_slot[g - 1][:], y[:], COPY, scale=gate_cols[:, g - 1 : g])
 
         def rest_rows(n, b):
             y = bank(b, [P, GROUPS - 1, P], f"y_back{n}")
@@ -272,8 +281,8 @@ def tile_moe_res_mlp_relu_kernel(
             engine.tensor_tensor(res[n][:, lo:hi], back[n][:, lo:hi], res[n][:, lo:hi], ADD)
             nc.sync.dma_start(out=out[n * P : (n + 1) * P, lo:hi], in_=res[n][:, lo:hi])
 
-        for g in (0, 1):
-            for s in range(last):
+        for s in range(last):
+            for g in (0, 1):
                 first(s, g)
         first(last, 0)
         activate(0)
@@ -284,19 +293,20 @@ def tile_moe_res_mlp_relu_kernel(
         activate(1)
         turn(1, 6)
         rest_rows_group0(6)
-        for s in range(PASSES):
-            first(s, 2)
+        for s in range(last):
+            for g in (2, 3):
+                first(s, g)
+        first(last, 2)
         activate(2)
         turn(2, 4)
         first_rows(1, 4)
-        for s in range(PASSES):
-            first(s, 3)
+        first(last, 3)
         activate(3)
         turn(3, 7)
         first_rows(2, 7)
         first_rows(3, 5)
         for g in range(1, GROUPS):
-            rest_by_slot(g)
+            rest_by_slot(g, g)
         add(nc.gpsimd, 0, 0, T)
         rest_rows(1, 0)
         add(nc.gpsimd, 1, 0, 512)

@@ -27,10 +27,10 @@ RELU = mybir.ActivationFunctionType.Relu
 MULT = mybir.AluOpType.mult
 ADD = mybir.AluOpType.add
 
-LOADS = [(0, 0, 512), (0, 512, T), (1, 0, 512), (1, 512, T), (2, 0, 512), (2, 512, T), (3, 0, 512), (3, 512, 896), (3, 896, T)]
+LOADS = [(0, 0, T), (1, 0, 512), (1, 512, T), (2, 0, 512), (2, 512, T), (3, 0, 512), (3, 512, 896), (3, 896, T)]
 PIECES = [(0, 0, 512), (0, 512, T), (1, 0, 512), (1, 512, T), (2, 0, 512), (2, 512, T), (3, 0, 256), (3, 256, 512), (3, 512, 768), (3, 768, T)]
 CASTS = [
-    (0, 0, 176, 512), (0, 512, 688, T),
+    (0, 512, 512, T), (0, 0, 352, 512),
     (1, 0, 512, 512), (1, 512, 768, T),
     (2, 0, 512, 512), (2, 512, 768, T),
     (3, 0, 256, 256), (3, 256, 384, 512), (3, 512, 768, 768), (3, 768, 768, 896), (3, 896, 952, T),
@@ -58,7 +58,7 @@ def tile_moe_res_mlp_relu_kernel(
         offsets = keep.tile([P, S // 16], U16, name="offsets")
         w1s = sb([P, E, PASSES * H], U8, "w1s")
         w2s = sb([P, E, N], U8, "w2s")
-        w1 = [[sb([P, 2, 2 * H], U8, f"w1_{e}_{a}") for a in range(2)] for e in range(E)]
+        w1 = {}
         w2 = sb([P, E, 2 * N], U8, "w2")
         gate_four = sb([P, 4], F32, "gate_four")
         gate_cols = sb([P, GROUPS - 1], F32, "gate_cols")
@@ -82,10 +82,10 @@ def tile_moe_res_mlp_relu_kernel(
         back = [sb([P, T], F32, f"back{n}") for n in range(N_TILES)]
         res = [sb([P, T], F32, f"res{n}") for n in range(N_TILES)]
 
+        nc.vector.memset(w2s[:].rearrange("p e i -> p (e i)").bitcast(I32), 0)
         for s in range(PASSES):
             nc.vector.memset(scales[s][:].bitcast(I32), 0)
         nc.vector.memset(w1s[:].rearrange("p e i -> p (e i)").bitcast(I32), 0)
-        nc.vector.memset(w2s[:].rearrange("p e i -> p (e i)").bitcast(I32), 0)
         nc.vector.memset(warm[:], 0.0)
         nc.scalar.activation(warm[:], warm[:], RELU)
         make_identity(nc, ident[:])
@@ -97,34 +97,42 @@ def tile_moe_res_mlp_relu_kernel(
             rows = xT[s * P * PACK : (s + 1) * P * PACK, t0:t1]
             nc.sync.dma_start(out=xf[i][:], in_=rows.rearrange("(p j) t -> p j t", j=PACK))
 
-        def load_w1(e, a):
+        def load_w1(e, s0, s1):
+            tile = sb([P, s1 - s0, 2 * H], U8, f"w1_{e}_{s0}")
             nc.sync.dma_start(
-                out=w1[e][a][:].bitcast(I32),
-                in_=w1_words[e, 2 * a : 2 * a + 2, :, :].bitcast(I32).rearrange("s p b -> p s b"),
+                out=tile[:].bitcast(I32), in_=w1_words[e, s0:s1, :, :].bitcast(I32).rearrange("s p b -> p s b")
             )
+            for s in range(s0, s1):
+                w1[e, s] = tile[:, s - s0, :]
+
+        def load_residual(n, lo, hi):
+            nc.sync.dma_start(out=res[n][:, lo:hi], in_=xr[n * P : (n + 1) * P, lo:hi])
 
         nc.sync.dma_start(out=gate_four[:], in_=gate[0, :].rearrange("(p f) -> p f", f=4))
         nc.sync.dma_start(offsets[:], offs)
-        for i in range(len(LOADS)):
+        for i in range(len(LOADS) - 3):
             load_x(i)
-        rows = w1_scales.bitcast(I32).rearrange("e s q i -> q (e s) i")
-        for r in range(4):
-            nc.sync.dma_start(
-                out=w1s[r:P:32, :, :].bitcast(I32).rearrange("q e (s i) -> q (e s) i", s=PASSES), in_=rows[r:16:4, :, :]
-            )
-        load_w1(0, 0)
-        load_w1(0, 1)
-        load_w1(1, 0)
-        load_w1(1, 1)
-        nc.sync.dma_start(out=w2[:].bitcast(I32), in_=w2_words[:, 0, :, :].bitcast(I32).rearrange("e p b -> p e b"))
         rows = w2_scales[:, 0, :, :].bitcast(I32)
         for r in range(4):
             nc.sync.dma_start(
                 out=w2s[r:P:32, :, :].bitcast(I32),
                 in_=rows[:, r:16:4, :].rearrange("e q i -> q e i"),
             )
-        for n in range(N_TILES):
-            nc.sync.dma_start(out=res[n][:], in_=xr[n * P : (n + 1) * P, :])
+        for i in range(len(LOADS) - 3, len(LOADS)):
+            load_x(i)
+        rows = w1_scales.bitcast(I32).rearrange("e s q i -> q (e s) i")
+        for r in range(4):
+            nc.sync.dma_start(
+                out=w1s[r:P:32, :, :].bitcast(I32).rearrange("q e (s i) -> q (e s) i", s=PASSES), in_=rows[r:16:4, :, :]
+            )
+        load_w1(0, 0, 2)
+        load_w1(0, 2, 4)
+        nc.sync.dma_start(out=w2[:].bitcast(I32), in_=w2_words[:, 0, :, :].bitcast(I32).rearrange("e p b -> p e b"))
+        load_w1(1, 0, 2)
+        load_residual(0, 0, T)
+        load_w1(1, 2, 4)
+        load_residual(1, 0, T)
+        load_residual(2, 0, T)
 
         spread_gate = bank(4, [P, 4, P], "spread_gate")
         for f in range(4):
@@ -181,7 +189,7 @@ def tile_moe_res_mlp_relu_kernel(
                 out=acc[g][:],
                 lhsT=picked[s, g][0].bitcast(E4M3),
                 lhsT_scale=picked[s, g][1],
-                rhs=w1[e][s // 2][:, s % 2, :].bitcast(E2M1),
+                rhs=w1[e, s].bitcast(E2M1),
                 rhs_scale=w1s[:, e, s * H : (s + 1) * H],
                 start=(s == 0),
                 stop=(s == PASSES - 1),
@@ -209,7 +217,7 @@ def tile_moe_res_mlp_relu_kernel(
                     sums = acc[0][:].rearrange("p (r w e) -> p w r e", w=2, e=2)[:, w, :, :]
                     nc.scalar.activation(h0[w][:].rearrange("p (r e) -> p r e", e=2), sums, RELU)
                 return
-            h[g] = sb([P, H], BF16, f"h{g}")
+            h[g] = at(3072, [P, H], BF16, "h3") if g == 3 else sb([P, H], BF16, f"h{g}")
             nc.scalar.activation(
                 h[g][:].rearrange("p (w r e) -> p w r e", w=2, e=2),
                 acc[g][:].rearrange("p (r w e) -> p w r e", w=2, e=2),
@@ -242,7 +250,7 @@ def tile_moe_res_mlp_relu_kernel(
         def first_rows(g, b):
             y = bank(b, [P, P], f"y{g}")
             second(g, 0, y[:])
-            y_first = sb([P, P], F32, f"y_first{g}")
+            y_first = at(3072, [P, P], F32, "y_first2") if g == 2 else sb([P, P], F32, f"y_first{g}")
             nc.scalar.copy(out=y_first[:], in_=y[:])
             lo, hi = g * P, (g + 1) * P
             nc.vector.tensor_tensor(back[0][:].indirect(listed(lo, hi)), y_first[:], gates[:, lo:hi], MULT)
@@ -281,14 +289,16 @@ def tile_moe_res_mlp_relu_kernel(
             engine.tensor_tensor(res[n][:, lo:hi], back[n][:, lo:hi], res[n][:, lo:hi], ADD)
             nc.sync.dma_start(out=out[n * P : (n + 1) * P, lo:hi], in_=res[n][:, lo:hi])
 
-        for s in range(last):
+        for s in range(2):
             for g in (0, 1):
                 first(s, g)
+        first(2, 0)
         first(last, 0)
         activate(0)
         turn(0, 4)
         pick(last, C + P, S, 2048)
         first_rows(0, 5)
+        first(2, 1)
         first(last, 1)
         activate(1)
         turn(1, 6)
@@ -299,16 +309,17 @@ def tile_moe_res_mlp_relu_kernel(
         first(last, 2)
         activate(2)
         turn(2, 4)
-        first_rows(1, 4)
+        first_rows(1, 0)
         first(last, 3)
         activate(3)
         turn(3, 7)
-        first_rows(2, 7)
+        first_rows(2, 1)
         first_rows(3, 5)
-        for g in range(1, GROUPS):
-            rest_by_slot(g, g)
+        rest_by_slot(1, 4)
+        rest_by_slot(2, 7)
+        rest_by_slot(3, 3)
         add(nc.gpsimd, 0, 0, T)
-        rest_rows(1, 0)
+        rest_rows(1, 2)
         add(nc.gpsimd, 1, 0, 512)
         add(nc.gpsimd, 1, 512, T)
         rest_rows(2, 6)

@@ -63,7 +63,6 @@ def tile_moe_res_mlp_relu_kernel(
         gate_four = sb([P, 4], F32, "gate_four")
         gate_cols = sb([P, GROUPS - 1], F32, "gate_cols")
         gates = sb([P, S], F32, "gates")
-        warm = sb([P, 8], F32, "warm")
         ident = sb([P, P], F32, "ident")
         xf = [sb([P, PACK, x[2] - x[1]], F32, f"xf{i}") for i, x in enumerate(LOADS)]
         xb = [sb([P, x[2] - x[1], PACK], BF16, f"xb{i}") for i, x in enumerate(PIECES[:-1])]
@@ -86,8 +85,6 @@ def tile_moe_res_mlp_relu_kernel(
         for s in range(PASSES):
             nc.vector.memset(scales[s][:].bitcast(I32), 0)
         nc.vector.memset(w1s[:].rearrange("p e i -> p (e i)").bitcast(I32), 0)
-        nc.vector.memset(warm[:], 0.0)
-        nc.scalar.activation(warm[:], warm[:], RELU)
         make_identity(nc, ident[:])
         for n in range(N_TILES):
             nc.gpsimd.memset(back[n][:], 0.0)

@@ -32,8 +32,8 @@ PIECES = [(0, 0, 512), (0, 512, T), (1, 0, 512), (1, 512, T), (2, 0, 512), (2, 5
 CASTS = [
     (0, 512, 512, T), (0, 0, 352, 512),
     (1, 0, 512, 512), (1, 512, 768, T),
-    (2, 0, 512, 512), (2, 512, 768, T),
-    (3, 0, 256, 256), (3, 256, 384, 512), (3, 512, 768, 768), (3, 768, 768, 896), (3, 896, 952, T),
+    (2, 0, 512, 512), (2, 512, 704, T),
+    (3, 0, 256, 256), (3, 256, 384, 512), (3, 512, 640, 768), (3, 768, 768, 896), (3, 896, 952, T),
 ]
 
 

@@ -27,6 +27,7 @@ RELU = mybir.ActivationFunctionType.Relu
 MULT = mybir.AluOpType.mult
 ADD = mybir.AluOpType.add
 
+ORDER = [(0, 1, 2, 3), (0, 1, 2, 3), (0, 1, 2, 3), (0, 1, 3, 2)]
 LOADS = [(0, 0, T), (1, 0, 512), (1, 512, T), (2, 0, 512), (2, 512, T), (3, 0, 512), (3, 512, 896), (3, 896, T)]
 PIECES = [(0, 0, 512), (0, 512, T), (1, 0, 512), (1, 512, T), (2, 0, 512), (2, 512, T), (3, 0, 256), (3, 256, 512), (3, 512, 768), (3, 768, T)]
 CASTS = [
@@ -56,10 +57,20 @@ def tile_moe_res_mlp_relu_kernel(
             return psum.tile(shape, F32, name=name, tag=f"bank{b}", bufs=1)
 
         offsets = keep.tile([P, S // 16], U16, name="offsets")
-        w1s = sb([P, E, PASSES * H], U8, "w1s")
+        w1s = [sb([P, PASSES * H], U8, f"w1s{e}") for e in range(E)]
         w2s = sb([P, E, N], U8, "w2s")
         w1 = {}
-        w2 = sb([P, E, 2 * N], U8, "w2")
+        w2_first = sb([P, 2 * P], U8, "w2_first")
+        w2_rest = sb([P, 2 * (N - P)], U8, "w2_rest")
+        w2_other = sb([P, 2 * N], U8, "w2_other")
+
+        def w2(e, lo, hi):
+            if e == 1:
+                return w2_other[:, 2 * lo : 2 * hi].bitcast(E2M1)
+            if hi <= P:
+                return w2_first[:, 2 * lo : 2 * hi].bitcast(E2M1)
+            return w2_rest[:, 2 * (lo - P) : 2 * (hi - P)].bitcast(E2M1)
+
         gate_four = sb([P, 4], F32, "gate_four")
         gate_cols = sb([P, GROUPS - 1], F32, "gate_cols")
         gates = sb([P, S], F32, "gates")
@@ -70,21 +81,23 @@ def tile_moe_res_mlp_relu_kernel(
         words = [sb([P, T], U32, f"words{s}") for s in range(PASSES)]
         scales = [sb([P, T], U8, f"scales{s}") for s in range(PASSES)]
         picked = {}
+        whole = {}
         h = {}
         h0 = [sb([P, H // 2], BF16, "h0_0"), sb([P, H // 2], BF16, "h0_1")]
         hg = [turns.tile([P, P, PACK], BF16, name="hg0", align_bytes=64, offset=2048)]
         hg.extend(sb([P, P, PACK], BF16, f"hg{g}") for g in range(1, GROUPS))
-        hq = [sb([P, P], U32, f"hq{g}") for g in range(GROUPS)]
+        hq = [at(3072, [P, P], U32, "hq0")]
+        hq.extend(sb([P, P], U32, f"hq{g}") for g in range(1, GROUPS))
         hs = [sb([P, P], U8, f"hs{g}") for g in range(GROUPS)]
-        y_slot = [sb([P, 2 * P], F32, f"y_slot{g}") for g in range(1, GROUPS)]
-        y_gated = [sb([P, S - P], F32, f"y_gated{n}") for n in range(1, N_TILES)]
+        y_slot = {}
         back = [sb([P, T], F32, f"back{n}") for n in range(N_TILES)]
         res = [sb([P, T], F32, f"res{n}") for n in range(N_TILES)]
 
         nc.vector.memset(w2s[:].rearrange("p e i -> p (e i)").bitcast(I32), 0)
         for s in range(PASSES):
             nc.vector.memset(scales[s][:].bitcast(I32), 0)
-        nc.vector.memset(w1s[:].rearrange("p e i -> p (e i)").bitcast(I32), 0)
+        for e in range(E):
+            nc.vector.memset(w1s[e][:].bitcast(I32), 0)
         make_identity(nc, ident[:])
         for n in range(N_TILES):
             nc.gpsimd.memset(back[n][:], 0.0)
@@ -105,31 +118,41 @@ def tile_moe_res_mlp_relu_kernel(
         def load_residual(n, lo, hi):
             nc.sync.dma_start(out=res[n][:, lo:hi], in_=xr[n * P : (n + 1) * P, lo:hi])
 
-        nc.sync.dma_start(out=gate_four[:], in_=gate[0, :].rearrange("(p f) -> p f", f=4))
+        def load_w1_scales(e):
+            rows = w1_scales[e].bitcast(I32).rearrange("s q i -> q s i")
+            for r in range(4):
+                nc.sync.dma_start(
+                    out=w1s[e][r:P:32, :].bitcast(I32).rearrange("q (s i) -> q s i", s=PASSES), in_=rows[r:16:4, :, :]
+                )
+
+        def load_w2_scales():
+            rows = w2_scales[:, 0, :, :].bitcast(I32)
+            for r in range(4):
+                nc.sync.dma_start(
+                    out=w2s[r:P:32, :, :].bitcast(I32),
+                    in_=rows[:, r:16:4, :].rearrange("e q i -> q e i"),
+                )
+
+        load_x(0)
         nc.sync.dma_start(offsets[:], offs)
-        for i in range(len(LOADS) - 3):
+        nc.sync.dma_start(out=gate_four[:], in_=gate[0, :].rearrange("(p f) -> p f", f=4))
+        for i in range(1, len(LOADS) - 3):
             load_x(i)
-        rows = w2_scales[:, 0, :, :].bitcast(I32)
-        for r in range(4):
-            nc.sync.dma_start(
-                out=w2s[r:P:32, :, :].bitcast(I32),
-                in_=rows[:, r:16:4, :].rearrange("e q i -> q e i"),
-            )
-        for i in range(len(LOADS) - 3, len(LOADS)):
+        load_w2_scales()
+        load_x(len(LOADS) - 3)
+        nc.sync.dma_start(out=w2_first[:].bitcast(I32), in_=w2_words[0, 0, :, 0 : 2 * P].bitcast(I32))
+        for i in range(len(LOADS) - 2, len(LOADS)):
             load_x(i)
-        rows = w1_scales.bitcast(I32).rearrange("e s q i -> q (e s) i")
-        for r in range(4):
-            nc.sync.dma_start(
-                out=w1s[r:P:32, :, :].bitcast(I32).rearrange("q e (s i) -> q (e s) i", s=PASSES), in_=rows[r:16:4, :, :]
-            )
+        load_w1_scales(0)
         load_w1(0, 0, 2)
         load_w1(0, 2, 4)
-        nc.sync.dma_start(out=w2[:].bitcast(I32), in_=w2_words[:, 0, :, :].bitcast(I32).rearrange("e p b -> p e b"))
         load_w1(1, 0, 2)
-        load_residual(0, 0, T)
+        load_w1_scales(1)
+        nc.sync.dma_start(out=w2_rest[:].bitcast(I32), in_=w2_words[0, 0, :, 2 * P : 2 * N].bitcast(I32))
+        nc.sync.dma_start(out=w2_other[:].bitcast(I32), in_=w2_words[1, 0, :, :].bitcast(I32))
         load_w1(1, 2, 4)
-        load_residual(1, 0, T)
-        load_residual(2, 0, T)
+        for n in range(N_TILES):
+            load_residual(n, 0, T)
 
         spread_gate = bank(4, [P, 4, P], "spread_gate")
         for f in range(4):
@@ -140,7 +163,7 @@ def tile_moe_res_mlp_relu_kernel(
             nc.tensor.transpose(turned_gate[:, g - 1, :], gates[:, g * P : (g + 1) * P], ident[:])
         nc.scalar.copy(out=gate_cols[:], in_=turned_gate[:, :, 0])
 
-        acc = [bank(g, [P, H], f"acc{g}") for g in range(GROUPS)]
+        acc = {}
 
         def holder(parts, s, t):
             return [i for i, x in enumerate(parts) if x[0] == s and x[1] <= t < x[2]][0]
@@ -176,20 +199,21 @@ def tile_moe_res_mlp_relu_kernel(
                 gs = turns.tile([P, n], U8, name=f"gs{s}_{lo}", align_bytes=64, offset=offset + 4 * n)
             nc.vector.tensor_copy(gw[:], words[s][:].indirect(listed(lo, hi)))
             nc.vector.tensor_copy(gs[:], scales[s][:].indirect(listed(lo, hi)))
+            whole[s, lo] = (gw[:], gs[:])
             for g in range(lo // P, hi // P):
                 cols = slice(g * P - lo, (g + 1) * P - lo)
                 picked[s, g] = (gw[:, cols], gs[:, cols])
 
-        def first(s, g):
+        def first(s, g, start, stop):
             e = g // (C // P)
             nc.tensor.matmul_mx(
                 out=acc[g][:],
                 lhsT=picked[s, g][0].bitcast(E4M3),
                 lhsT_scale=picked[s, g][1],
                 rhs=w1[e, s].bitcast(E2M1),
-                rhs_scale=w1s[:, e, s * H : (s + 1) * H],
-                start=(s == 0),
-                stop=(s == PASSES - 1),
+                rhs_scale=w1s[e][:, s * H : (s + 1) * H],
+                start=start,
+                stop=stop,
             )
 
         last = PASSES - 1
@@ -214,7 +238,7 @@ def tile_moe_res_mlp_relu_kernel(
                     sums = acc[0][:].rearrange("p (r w e) -> p w r e", w=2, e=2)[:, w, :, :]
                     nc.scalar.activation(h0[w][:].rearrange("p (r e) -> p r e", e=2), sums, RELU)
                 return
-            h[g] = at(3072, [P, H], BF16, "h3") if g == 3 else sb([P, H], BF16, f"h{g}")
+            h[g] = sb([P, H], BF16, "h1") if g == 1 else at(1024 + 1024 * g, [P, H], BF16, f"h{g}")
             nc.scalar.activation(
                 h[g][:].rearrange("p (w r e) -> p w r e", w=2, e=2),
                 acc[g][:].rearrange("p (r w e) -> p w r e", w=2, e=2),
@@ -236,7 +260,7 @@ def tile_moe_res_mlp_relu_kernel(
             e = g // (C // P)
             nc.tensor.matmul_mx(
                 out=dst,
-                lhsT=w2[:, e, 2 * P * n : 2 * P * (n + 1)].bitcast(E2M1),
+                lhsT=w2(e, P * n, P * (n + 1)),
                 lhsT_scale=w2s[:, e, n * P : (n + 1) * P],
                 rhs=hq[g][:].bitcast(E4M3),
                 rhs_scale=hs[g][:],
@@ -244,81 +268,103 @@ def tile_moe_res_mlp_relu_kernel(
                 stop=True,
             )
 
-        def first_rows(g, b):
-            y = bank(b, [P, P], f"y{g}")
-            second(g, 0, y[:])
-            y_first = at(3072, [P, P], F32, "y_first2") if g == 2 else sb([P, P], F32, f"y_first{g}")
-            nc.scalar.copy(out=y_first[:], in_=y[:])
-            lo, hi = g * P, (g + 1) * P
-            nc.vector.tensor_tensor(back[0][:].indirect(listed(lo, hi)), y_first[:], gates[:, lo:hi], MULT)
+        def products(b, pairs):
+            y = bank(b, [P, len(pairs), P], "y%d_%d" % pairs[0])
+            for i, (g, n) in enumerate(pairs):
+                second(g, n, y[:, i, :])
+            return y
 
-        def rest_rows_group0(b):
-            y = bank(b, [P, 2, P], "y0_rest")
-            y_rest0 = sb([P, 2, P], F32, "y_rest0")
-            for n in (1, 2):
-                second(0, n, y[:, n - 1, :])
-            nc.scalar.copy(out=y_rest0[:], in_=y[:])
-            for n in (1, 2):
-                nc.vector.tensor_tensor(back[n][:].indirect(listed(0, P)), y_rest0[:, n - 1, :], gates[:, 0:P], MULT)
+        def leave(y, name, offset=None):
+            shape = [P, y.shape[1], P]
+            y_rows = sb(shape, F32, name) if offset is None else at(offset, shape, F32, name)
+            nc.scalar.copy(out=y_rows[:], in_=y)
+            return y_rows
 
-        def rest_by_slot(g, b):
+        def scatter(n, lo, hi, y_rows):
+            nc.vector.tensor_tensor(back[n][:].indirect(listed(lo, hi)), y_rows, gates[:, lo:hi], MULT)
+
+        def by_slot(g, n0, b):
             e = g // (C // P)
-            y = bank(b, [P, 2 * P], f"y_slot{g}")
+            width = N - n0 * P
+            y = bank(b, [P, width], f"y_slot{g}")
             nc.tensor.matmul_mx(
                 out=y[:],
                 lhsT=hq[g][:].bitcast(E4M3),
                 lhsT_scale=hs[g][:],
-                rhs=w2[:, e, 2 * P : 2 * N].bitcast(E2M1),
-                rhs_scale=w2s[:, e, P:N],
+                rhs=w2(e, n0 * P, N),
+                rhs_scale=w2s[:, e, n0 * P : N],
                 start=True,
                 stop=True,
             )
-            nc.scalar.activation(y_slot[g - 1][:], y[:], COPY, scale=gate_cols[:, g - 1 : g])
+            gated = sb([P, width], F32, f"gated{g}")
+            nc.scalar.activation(gated[:], y[:], COPY, scale=gate_cols[:, g - 1 : g])
+            for n in range(n0, N_TILES):
+                y_slot[g, n] = gated[:, (n - n0) * P : (n - n0 + 1) * P]
 
-        def rest_rows(n, b):
-            y = bank(b, [P, GROUPS - 1, P], f"y_back{n}")
-            for g in range(1, GROUPS):
-                nc.tensor.transpose(y[:, g - 1, :], y_slot[g - 1][:, (n - 1) * P : n * P], ident[:])
-            nc.scalar.copy(out=y_gated[n - 1][:], in_=y[:].rearrange("p g r -> p (g r)"))
-            nc.vector.tensor_copy(back[n][:].indirect(listed(P, S)), y_gated[n - 1][:])
+        def rest_rows(n, g0, b):
+            y = bank(b, [P, GROUPS - g0, P], f"y_back{n}")
+            for g in range(g0, GROUPS):
+                nc.tensor.transpose(y[:, g - g0, :], y_slot[g, n], ident[:])
+            y_gated = sb([P, S - g0 * P], F32, f"y_gated{n}")
+            nc.scalar.copy(out=y_gated[:], in_=y[:].rearrange("p g r -> p (g r)"))
+            nc.vector.tensor_copy(back[n][:].indirect(listed(g0 * P, S)), y_gated[:])
+
+        def passes(g, order):
+            for s in order:
+                first(s, g, s == ORDER[g][0], s == ORDER[g][-1])
 
         def add(engine, n, lo, hi):
             engine.tensor_tensor(res[n][:, lo:hi], back[n][:, lo:hi], res[n][:, lo:hi], ADD)
             nc.sync.dma_start(out=out[n * P : (n + 1) * P, lo:hi], in_=res[n][:, lo:hi])
 
-        for s in range(2):
-            for g in (0, 1):
-                first(s, g)
-        first(2, 0)
-        first(last, 0)
+        for i in range(4):
+            idle = bank(6 + i % 2, [P, S], f"idle{i}")
+            nc.tensor.matmul_mx(
+                out=idle[:],
+                lhsT=w2(0, 0, P),
+                lhsT_scale=w2s[:, 0, 0:P],
+                rhs=whole[0, 0][0].bitcast(E4M3),
+                rhs_scale=whole[0, 0][1],
+                start=True,
+                stop=True,
+            )
+        acc[0] = bank(0, [P, H], "acc0")
+        acc[1] = bank(1, [P, H], "acc1")
+        acc[3] = bank(2, [P, H], "acc3")
+        passes(0, ORDER[0])
         activate(0)
         turn(0, 4)
         pick(last, C + P, S, 2048)
-        first_rows(0, 5)
-        first(2, 1)
-        first(last, 1)
+        passes(1, ORDER[1])
         activate(1)
-        turn(1, 6)
-        rest_rows_group0(6)
-        for s in range(last):
-            for g in (2, 3):
-                first(s, g)
-        first(last, 2)
+        turn(1, 5)
+        y00 = leave(products(0, [(0, 0)])[:], "y00")
+        scatter(0, 0, P, y00[:, 0, :])
+        y0 = products(3, [(0, 1), (0, 2)])
+        y01 = leave(y0[:, 0:1, :], "y01")
+        scatter(1, 0, P, y01[:, 0, :])
+        y1 = leave(products(4, [(1, 0), (1, 1)])[:], "y1")
+        scatter(0, P, C, y1[:, 0, :])
+        scatter(1, P, C, y1[:, 1, :])
+        acc[2] = bank(1, [P, H], "acc2")
+        passes(2, ORDER[2])
         activate(2)
-        turn(2, 4)
-        first_rows(1, 0)
-        first(last, 3)
+        passes(3, ORDER[3])
         activate(3)
-        turn(3, 7)
-        first_rows(2, 1)
-        first_rows(3, 5)
-        rest_by_slot(1, 4)
-        rest_by_slot(2, 7)
-        rest_by_slot(3, 3)
+        turn(2, 6)
+        turn(3, 5)
+        y02 = leave(y0[:, 1:2, :], "y02", 4096)
+        scatter(2, 0, P, y02[:, 0, :])
+        by_slot(1, 2, 2)
+        y23 = leave(products(0, [(2, 0), (3, 0)])[:], "y23")
+        scatter(0, C, S, y23[:].rearrange("p g r -> p (g r)"))
+        by_slot(2, 1, 1)
+        by_slot(3, 1, 2)
         add(nc.gpsimd, 0, 0, T)
-        rest_rows(1, 2)
-        add(nc.gpsimd, 1, 0, 512)
-        add(nc.gpsimd, 1, 512, T)
-        rest_rows(2, 6)
+        rest_rows(1, 2, 3)
+        add(nc.gpsimd, 1, 0, 384)
+        add(nc.gpsimd, 1, 384, 768)
+        rest_rows(2, 1, 7)
+        add(nc.vector, 1, 768, T)
         for lo in range(0, T, 256):
             add(nc.vector, 2, lo, lo + 256)

@@ -27,14 +27,17 @@ RELU = mybir.ActivationFunctionType.Relu
 MULT = mybir.AluOpType.mult
 ADD = mybir.AluOpType.add
 
-ORDER = [(0, 1, 2, 3), (0, 1, 2, 3), (0, 1, 2, 3), (0, 1, 3, 2)]
-LOADS = [(0, 0, T), (1, 0, 512), (1, 512, T), (2, 0, 512), (2, 512, T), (3, 0, 512), (3, 512, 896), (3, 896, T)]
-PIECES = [(0, 0, 512), (0, 512, T), (1, 0, 512), (1, 512, T), (2, 0, 512), (2, 512, T), (3, 0, 256), (3, 256, 512), (3, 512, 768), (3, 768, T)]
+ORDER = [(0, 1, 2, 3), (0, 1, 2, 3), (0, 1, 2, 3), (0, 1, 2, 3)]
+LOADS = [(0, 0, 512), (0, 512, T), (1, 0, 512), (1, 512, T), (2, 0, 512), (2, 512, T), (3, 0, 512), (3, 512, 896), (3, 896, T)]
+PIECES = [
+    (0, 0, 512), (0, 512, T), (1, 0, 512), (1, 512, T), (2, 0, 512), (2, 512, T),
+    (3, 0, 256), (3, 256, 512), (3, 512, 768), (3, 768, 896), (3, 896, T),
+]
 CASTS = [
-    (0, 512, 512, T), (0, 0, 352, 512),
+    (0, 0, 192, 512), (0, 512, 704, T),
     (1, 0, 512, 512), (1, 512, 768, T),
-    (2, 0, 512, 512), (2, 512, 704, T),
-    (3, 0, 256, 256), (3, 256, 384, 512), (3, 512, 640, 768), (3, 768, 768, 896), (3, 896, 952, T),
+    (2, 0, 512, 512), (2, 512, 768, T),
+    (3, 0, 256, 256), (3, 256, 384, 512), (3, 512, 640, 768), (3, 768, 768, 896), (3, 896, 976, T),
 ]
 
 
@@ -195,8 +198,8 @@ def tile_moe_res_mlp_relu_kernel(
             if offset is None:
                 gw, gs = sb([P, n], U32, f"gw{s}_{lo}"), sb([P, n], U8, f"gs{s}_{lo}")
             else:
-                gw = turns.tile([P, n], U32, name=f"gw{s}_{lo}", align_bytes=64, offset=offset)
-                gs = turns.tile([P, n], U8, name=f"gs{s}_{lo}", align_bytes=64, offset=offset + 4 * n)
+                gw = turns.tile([P, n], U32, name=f"gw{s}_{lo}", align_bytes=64, offset=offset + n)
+                gs = turns.tile([P, n], U8, name=f"gs{s}_{lo}", align_bytes=64, offset=offset)
             nc.vector.tensor_copy(gw[:], words[s][:].indirect(listed(lo, hi)))
             nc.vector.tensor_copy(gs[:], scales[s][:].indirect(listed(lo, hi)))
             whole[s, lo] = (gw[:], gs[:])
@@ -309,6 +312,21 @@ def tile_moe_res_mlp_relu_kernel(
             nc.scalar.copy(out=y_gated[:], in_=y[:].rearrange("p g r -> p (g r)"))
             nc.vector.tensor_copy(back[n][:].indirect(listed(g0 * P, S)), y_gated[:])
 
+        def add_turned(n, lo, hi, b_there, b_back):
+            chunks = (hi - lo) // P
+            there = bank(b_there, [P, chunks, P], f"sum_there{n}")
+            for c in range(chunks):
+                cols = slice(lo + c * P, lo + (c + 1) * P)
+                nc.tensor.matmul(there[:, c, :], res[n][:, cols], ident[:], start=True, stop=False, is_transpose=True)
+                nc.tensor.matmul(there[:, c, :], back[n][:, cols], ident[:], start=False, stop=True, is_transpose=True)
+            by_token = sb([P, chunks, P], F32, f"sum_by_token{n}")
+            nc.scalar.copy(out=by_token[:], in_=there[:])
+            again = bank(b_back, [P, chunks * P], f"sum_again{n}")
+            for c in range(chunks):
+                nc.tensor.transpose(again[:, c * P : (c + 1) * P], by_token[:, c, :], ident[:])
+            nc.scalar.copy(out=res[n][:, lo:hi], in_=again[:])
+            nc.scalar.dma_start(out=out[n * P : (n + 1) * P, lo:hi], in_=res[n][:, lo:hi])
+
         def passes(g, order):
             for s in order:
                 first(s, g, s == ORDER[g][0], s == ORDER[g][-1])
@@ -352,19 +370,22 @@ def tile_moe_res_mlp_relu_kernel(
         passes(3, ORDER[3])
         activate(3)
         turn(2, 6)
-        turn(3, 5)
-        y02 = leave(y0[:, 1:2, :], "y02", 4096)
+        y02 = leave(y0[:, 1:2, :], "y02", 3072)
         scatter(2, 0, P, y02[:, 0, :])
+        turn(3, 5)
+        y20 = leave(products(0, [(2, 0)])[:], "y20", 4096)
+        scatter(0, C, C + P, y20[:, 0, :])
         by_slot(1, 2, 2)
-        y23 = leave(products(0, [(2, 0), (3, 0)])[:], "y23")
-        scatter(0, C, S, y23[:].rearrange("p g r -> p (g r)"))
+        y30 = leave(products(4, [(3, 0)])[:], "y30")
+        scatter(0, C + P, S, y30[:, 0, :])
         by_slot(2, 1, 1)
         by_slot(3, 1, 2)
-        add(nc.gpsimd, 0, 0, T)
+        add(nc.gpsimd, 0, 0, 512)
         rest_rows(1, 2, 3)
         add(nc.gpsimd, 1, 0, 384)
         add(nc.gpsimd, 1, 384, 768)
         rest_rows(2, 1, 7)
-        add(nc.vector, 1, 768, T)
+        add_turned(0, 512, T, 3, 7)
+        add_turned(1, 768, T, 0, 1)
         for lo in range(0, T, 256):
             add(nc.vector, 2, lo, lo + 256)

@@ -335,17 +335,6 @@ def tile_moe_res_mlp_relu_kernel(
             engine.tensor_tensor(res[n][:, lo:hi], back[n][:, lo:hi], res[n][:, lo:hi], ADD)
             nc.sync.dma_start(out=out[n * P : (n + 1) * P, lo:hi], in_=res[n][:, lo:hi])
 
-        for i in range(4):
-            idle = bank(6 + i % 2, [P, S], f"idle{i}")
-            nc.tensor.matmul_mx(
-                out=idle[:],
-                lhsT=w2(0, 0, P),
-                lhsT_scale=w2s[:, 0, 0:P],
-                rhs=whole[0, 0][0].bitcast(E4M3),
-                rhs_scale=whole[0, 0][1],
-                start=True,
-                stop=True,
-            )
         acc[0] = bank(0, [P, H], "acc0")
         acc[1] = bank(1, [P, H], "acc1")
         acc[3] = bank(2, [P, H], "acc3")

@@ -27,14 +27,14 @@ RELU = mybir.ActivationFunctionType.Relu
 MULT = mybir.AluOpType.mult
 ADD = mybir.AluOpType.add
 
-ORDER = [(0, 1, 2, 3), (0, 1, 2, 3), (0, 1, 2, 3), (0, 1, 2, 3)]
-LOADS = [(0, 0, 512), (0, 512, T), (1, 0, 512), (1, 512, T), (2, 0, 512), (2, 512, T), (3, 0, 512), (3, 512, 896), (3, 896, T)]
+ORDER = [(0, 1, 2, 3), (0, 1, 2, 3), (0, 1, 2, 3), (0, 1, 3, 2)]
+LOADS = [(0, 0, T), (1, 0, 512), (1, 512, T), (2, 0, 512), (2, 512, T), (3, 0, 512), (3, 512, 896), (3, 896, T)]
 PIECES = [
     (0, 0, 512), (0, 512, T), (1, 0, 512), (1, 512, T), (2, 0, 512), (2, 512, T),
     (3, 0, 256), (3, 256, 512), (3, 512, 768), (3, 768, 896), (3, 896, T),
 ]
 CASTS = [
-    (0, 0, 192, 512), (0, 512, 704, T),
+    (0, 512, 512, T), (0, 0, 384, 512),
     (1, 0, 512, 512), (1, 512, 768, T),
     (2, 0, 512, 512), (2, 512, 768, T),
     (3, 0, 256, 256), (3, 256, 384, 512), (3, 512, 640, 768), (3, 768, 768, 896), (3, 896, 976, T),
@@ -152,8 +152,8 @@ def tile_moe_res_mlp_relu_kernel(
         load_w1(1, 0, 2)
         load_w1_scales(1)
         nc.sync.dma_start(out=w2_rest[:].bitcast(I32), in_=w2_words[0, 0, :, 2 * P : 2 * N].bitcast(I32))
-        nc.sync.dma_start(out=w2_other[:].bitcast(I32), in_=w2_words[1, 0, :, :].bitcast(I32))
         load_w1(1, 2, 4)
+        nc.sync.dma_start(out=w2_other[:].bitcast(I32), in_=w2_words[1, 0, :, :].bitcast(I32))
         for n in range(N_TILES):
             load_residual(n, 0, T)
 
@@ -359,14 +359,12 @@ def tile_moe_res_mlp_relu_kernel(
         passes(3, ORDER[3])
         activate(3)
         turn(2, 6)
-        y02 = leave(y0[:, 1:2, :], "y02", 3072)
-        scatter(2, 0, P, y02[:, 0, :])
         turn(3, 5)
-        y20 = leave(products(0, [(2, 0)])[:], "y20", 4096)
-        scatter(0, C, C + P, y20[:, 0, :])
+        y02 = leave(y0[:, 1:2, :], "y02", 4096)
+        scatter(2, 0, P, y02[:, 0, :])
         by_slot(1, 2, 2)
-        y30 = leave(products(4, [(3, 0)])[:], "y30")
-        scatter(0, C + P, S, y30[:, 0, :])
+        y23 = leave(products(0, [(2, 0), (3, 0)])[:], "y23")
+        scatter(0, C, S, y23[:].rearrange("p g r -> p (g r)"))
         by_slot(2, 1, 1)
         by_slot(3, 1, 2)
         add(nc.gpsimd, 0, 0, 512)

@@ -27,18 +27,12 @@ RELU = mybir.ActivationFunctionType.Relu
 MULT = mybir.AluOpType.mult
 ADD = mybir.AluOpType.add
 
-ORDER = [(0, 1, 2, 3), (0, 1, 2, 3), (0, 1, 2, 3), (0, 1, 3, 2)]
-LOADS = [(0, 0, T), (1, 0, 512), (1, 512, T), (2, 0, 512), (2, 512, T), (3, 0, 512), (3, 512, 896), (3, 896, T)]
-PIECES = [
-    (0, 0, 512), (0, 512, T), (1, 0, 512), (1, 512, T), (2, 0, 512), (2, 512, T),
-    (3, 0, 256), (3, 256, 512), (3, 512, 768), (3, 768, 896), (3, 896, T),
+LOADS = [
+    (0, 0, 0, 384, T), (0, 1, 0, 640, T), (1, 0, 0, 896, T), (1, 1, 0, T, T),
+    (2, 0, 0, T, T), (2, 1, 0, 896, T), (3, 0, 0, 512, T),
+    (3, 1, 0, 512, 512), (3, 1, 512, 640, 896), (3, 1, 896, 960, T),
 ]
-CASTS = [
-    (0, 512, 512, T), (0, 0, 384, 512),
-    (1, 0, 512, 512), (1, 512, 768, T),
-    (2, 0, 512, 512), (2, 512, 768, T),
-    (3, 0, 256, 256), (3, 256, 384, 512), (3, 512, 640, 768), (3, 768, 768, 896), (3, 896, 976, T),
-]
+XF_BYTES = 8 * T
 
 
 def tile_moe_res_mlp_relu_kernel(
@@ -78,13 +72,15 @@ def tile_moe_res_mlp_relu_kernel(
         gate_cols = sb([P, GROUPS - 1], F32, "gate_cols")
         gates = sb([P, S], F32, "gates")
         ident = sb([P, P], F32, "ident")
-        xf = [sb([P, PACK, x[2] - x[1]], F32, f"xf{i}") for i, x in enumerate(LOADS)]
-        xb = [sb([P, x[2] - x[1], PACK], BF16, f"xb{i}") for i, x in enumerate(PIECES[:-1])]
-        xb.append(turns.tile([P, PIECES[-1][2] - PIECES[-1][1], PACK], BF16, name="xb_last", align_bytes=64, offset=0))
-        words = [sb([P, T], U32, f"words{s}") for s in range(PASSES)]
-        scales = [sb([P, T], U8, f"scales{s}") for s in range(PASSES)]
+        stage = ctx.enter_context(tc.tile_pool(name="stage", bufs=1))
+        xf = [
+            stage.tile([P, 2 * (x[4] - x[2])], F32, name=f"xf{i}", align_bytes=64, offset=min(i, 7) * XF_BYTES + 8 * x[2])
+            for i, x in enumerate(LOADS)
+        ]
+        pairs_of = {(s, u): sb([P, T, 2], BF16, f"pairs{s}_{u}") for s in range(PASSES) for u in range(2)}
         picked = {}
-        whole = {}
+        woven = {}
+        codes = {}
         h = {}
         h0 = [sb([P, H // 2], BF16, "h0_0"), sb([P, H // 2], BF16, "h0_1")]
         hg = [turns.tile([P, P, PACK], BF16, name="hg0", align_bytes=64, offset=2048)]
@@ -97,8 +93,6 @@ def tile_moe_res_mlp_relu_kernel(
         res = [sb([P, T], F32, f"res{n}") for n in range(N_TILES)]
 
         nc.vector.memset(w2s[:].rearrange("p e i -> p (e i)").bitcast(I32), 0)
-        for s in range(PASSES):
-            nc.vector.memset(scales[s][:].bitcast(I32), 0)
         for e in range(E):
             nc.vector.memset(w1s[e][:].bitcast(I32), 0)
         make_identity(nc, ident[:])
@@ -106,9 +100,12 @@ def tile_moe_res_mlp_relu_kernel(
             nc.gpsimd.memset(back[n][:], 0.0)
 
         def load_x(i):
-            s, t0, t1 = LOADS[i]
+            s, u, t0, cut, t1 = LOADS[i]
             rows = xT[s * P * PACK : (s + 1) * P * PACK, t0:t1]
-            nc.sync.dma_start(out=xf[i][:], in_=rows.rearrange("(p j) t -> p j t", j=PACK))
+            nc.sync.dma_start(
+                out=xf[i][:].rearrange("p (e t) -> p e t", e=2),
+                in_=rows.rearrange("(p u e) t -> p u e t", u=2, e=2)[:, u, :, :],
+            )
 
         def load_w1(e, s0, s1):
             tile = sb([P, s1 - s0, 2 * H], U8, f"w1_{e}_{s0}")
@@ -168,51 +165,59 @@ def tile_moe_res_mlp_relu_kernel(
 
         acc = {}
 
-        def holder(parts, s, t):
-            return [i for i, x in enumerate(parts) if x[0] == s and x[1] <= t < x[2]][0]
-
-        def cast(s, lo, hi, on_scalar):
-            if lo == hi:
-                return
-            a, b = holder(LOADS, s, lo), holder(PIECES, s, lo)
-            dst = xb[b][:, lo - PIECES[b][1] : hi - PIECES[b][1], :].rearrange("p (c i) j -> p c j i", i=4)
-            src = xf[a][:, :, lo - LOADS[a][1] : hi - LOADS[a][1]].rearrange("p j (c i) -> p c j i", i=4)
-            if on_scalar:
-                nc.scalar.activation(dst, src, COPY)
-            else:
-                nc.vector.tensor_copy(out=dst, in_=src)
-
-        def quantise(i):
-            s, t0, t1 = PIECES[i]
-            nc.vector.quantize_mx(
-                out=words[s][:, t0:t1].bitcast(E4M3),
-                scales=scales[s][:, t0:t1],
-                in_=xb[i][:].rearrange("p t j -> p (t j)"),
-            )
+        def cast(i):
+            s, u, t0, cut, t1 = LOADS[i]
+            src = xf[i][:].rearrange("p (e t) -> p t e", e=2)
+            nc.scalar.activation(pairs_of[s, u][:, t0:cut, :], src[:, 0 : cut - t0, :], COPY)
+            if cut < t1:
+                nc.vector.tensor_copy(out=pairs_of[s, u][:, cut:t1, :], in_=src[:, cut - t0 : t1 - t0, :])
 
         def listed(lo, hi):
             return offsets[:, lo // 16 : hi // 16]
 
-        def pick(s, lo, hi, offset=None):
-            n = hi - lo
+        def window(s, u):
+            return pairs_of[s, u][:].rearrange("p t e -> p (t e)").bitcast(U32)
+
+        def room(offset, n, name):
             if offset is None:
-                gw, gs = sb([P, n], U32, f"gw{s}_{lo}"), sb([P, n], U8, f"gs{s}_{lo}")
+                return sb([P, n], U32, name)[:]
+            return stage.tile([P, n], U32, name=name, align_bytes=64, offset=offset)[:]
+
+        def weave(s, lo, hi, on_scalar, offset=None):
+            woven[s, lo] = room(offset, 2 * (hi - lo), f"woven{s}_{lo}")
+            dst = woven[s, lo].rearrange("p (n u) -> p n u", u=2)
+            src = picked[s][:, :, lo:hi].rearrange("p u n -> p n u")
+            if on_scalar:
+                nc.scalar.copy(out=dst, in_=src)
             else:
-                gw = turns.tile([P, n], U32, name=f"gw{s}_{lo}", align_bytes=64, offset=offset + n)
-                gs = turns.tile([P, n], U8, name=f"gs{s}_{lo}", align_bytes=64, offset=offset)
-            nc.vector.tensor_copy(gw[:], words[s][:].indirect(listed(lo, hi)))
-            nc.vector.tensor_copy(gs[:], scales[s][:].indirect(listed(lo, hi)))
-            whole[s, lo] = (gw[:], gs[:])
+                nc.vector.tensor_copy(out=dst.bitcast(I32), in_=src.bitcast(I32))
+
+        def pick_plain(s, u, lo, hi):
+            if s not in picked:
+                picked[s] = sb([P, 2, S], U32, f"picked{s}")
+            nc.vector.tensor_copy(picked[s][:, u, lo:hi], window(s, u).indirect(listed(lo, hi)))
+
+        def pick_woven(s, u, lo, hi, offset=None):
+            if (s, lo) not in woven:
+                woven[s, lo] = room(offset, 2 * (hi - lo), f"woven{s}_{lo}")
+            nc.vector.tensor_copy(
+                woven[s, lo].rearrange("p (n u) -> p n u", u=2)[:, :, u], window(s, u).indirect(listed(lo, hi))
+            )
+
+        def quantise(s, lo, hi, offset=None):
+            words = room(offset, hi - lo, f"words{s}_{lo}")
+            scales = sb([P, hi - lo], U8, f"scales{s}_{lo}")
+            nc.vector.quantize_mx(out=words.bitcast(E4M3), scales=scales[:], in_=woven[s, lo].bitcast(BF16))
             for g in range(lo // P, hi // P):
                 cols = slice(g * P - lo, (g + 1) * P - lo)
-                picked[s, g] = (gw[:, cols], gs[:, cols])
+                codes[s, g] = (words[:, cols], scales[:, cols])
 
         def first(s, g, start, stop):
             e = g // (C // P)
             nc.tensor.matmul_mx(
                 out=acc[g][:],
-                lhsT=picked[s, g][0].bitcast(E4M3),
-                lhsT_scale=picked[s, g][1],
+                lhsT=codes[s, g][0].bitcast(E4M3),
+                lhsT_scale=codes[s, g][1],
                 rhs=w1[e, s].bitcast(E2M1),
                 rhs_scale=w1s[e][:, s * H : (s + 1) * H],
                 start=start,
@@ -220,20 +225,43 @@ def tile_moe_res_mlp_relu_kernel(
             )
 
         last = PASSES - 1
-        done = {}
-        for s, lo, cut, hi in CASTS:
-            cast(s, lo, cut, True)
-            cast(s, cut, hi, False)
-            i = holder(PIECES, s, lo)
-            if PIECES[i][2] == hi:
-                quantise(i)
-            done[s] = done.get(s, 0) + hi - lo
-            if done[s] == T and s < last:
-                pick(s, 0, S if s < last - 1 else C)
-        pick(last, 0, P)
-        pick(last, P, C)
-        pick(last - 1, C, S, 0)
-        pick(last, C, C + P)
+        spare = 8 * XF_BYTES
+        for s in range(last - 1):
+            cast(2 * s)
+            pick_plain(s, 0, 0, S)
+            cast(2 * s + 1)
+            for lo in (0, C):
+                pick_plain(s, 1, lo, lo + C)
+            for lo in (0, C):
+                weave(s, lo, lo + C, False)
+            for lo in (0, C):
+                quantise(s, lo, lo + C)
+        cast(2 * last - 2)
+        pick_plain(last - 1, 0, 0, S)
+        cast(2 * last - 1)
+        pick_plain(last - 1, 1, 0, C)
+        cast(2 * last)
+        weave(last - 1, 0, C, False, 2 * last * XF_BYTES)
+        pick_woven(last, 0, 0, P, spare)
+        pick_woven(last, 0, P, C, spare + 4096)
+        for i in range(2 * last + 1, len(LOADS)):
+            cast(i)
+        quantise(last - 1, 0, C, 8 * XF_BYTES - 1024)
+        pick_woven(last, 1, 0, P)
+        pick_woven(last, 1, P, C)
+        quantise(last, 0, P)
+        quantise(last, P, C)
+        late = stage.tile([P, 2, C], U32, name="late", align_bytes=64, offset=spare)
+        nc.vector.tensor_copy(late[:, 1, :], window(last - 1, 1).indirect(listed(C, S)))
+        nc.scalar.copy(out=late[:, 0, :], in_=picked[last - 1][:, 0, C:S])
+        woven[last - 1, C] = room(None, 2 * C, "woven_late")
+        nc.scalar.copy(
+            out=woven[last - 1, C].rearrange("p (n u) -> p n u", u=2), in_=late[:].rearrange("p u n -> p n u")
+        )
+        pick_woven(last, 0, C, S, spare + 4096)
+        pick_woven(last, 1, C, S)
+        quantise(last - 1, C, S)
+        quantise(last, C, S)
 
         def activate(g):
             if g == 0:
@@ -329,7 +357,7 @@ def tile_moe_res_mlp_relu_kernel(
 
         def passes(g, order):
             for s in order:
-                first(s, g, s == ORDER[g][0], s == ORDER[g][-1])
+                first(s, g, s == 0, s == last)
 
         def add(engine, n, lo, hi):
             engine.tensor_tensor(res[n][:, lo:hi], back[n][:, lo:hi], res[n][:, lo:hi], ADD)
@@ -338,11 +366,11 @@ def tile_moe_res_mlp_relu_kernel(
         acc[0] = bank(0, [P, H], "acc0")
         acc[1] = bank(1, [P, H], "acc1")
         acc[3] = bank(2, [P, H], "acc3")
-        passes(0, ORDER[0])
+        for s in range(PASSES):
+            passes(0, [s])
+            passes(1, [s])
         activate(0)
         turn(0, 4)
-        pick(last, C + P, S, 2048)
-        passes(1, ORDER[1])
         activate(1)
         turn(1, 5)
         y00 = leave(products(0, [(0, 0)])[:], "y00")
@@ -354,9 +382,9 @@ def tile_moe_res_mlp_relu_kernel(
         scatter(0, P, C, y1[:, 0, :])
         scatter(1, P, C, y1[:, 1, :])
         acc[2] = bank(1, [P, H], "acc2")
-        passes(2, ORDER[2])
+        passes(2, range(PASSES))
         activate(2)
-        passes(3, ORDER[3])
+        passes(3, range(PASSES))
         activate(3)
         turn(2, 6)
         turn(3, 5)

@@ -28,11 +28,10 @@ MULT = mybir.AluOpType.mult
 ADD = mybir.AluOpType.add
 
 LOADS = [
-    (0, 0, 0, 384, T), (0, 1, 0, 640, T), (1, 0, 0, 896, T), (1, 1, 0, T, T),
-    (2, 0, 0, T, T), (2, 1, 0, 896, T), (3, 0, 0, 512, T),
-    (3, 1, 0, 512, 512), (3, 1, 512, 640, 896), (3, 1, 896, 960, T),
+    (0, 0, 0, 384, T, T), (0, 1, 0, 640, T, T), (1, 0, 0, 768, 768, T), (1, 1, 0, 768, 768, T),
+    (2, 0, 0, 768, 768, T), (2, 1, 0, 768, 768, T), (3, 0, 0, 768, 768, T),
+    (3, 1, 0, 320, 320, 512), (3, 1, 512, 672, 672, 768), (3, 1, 768, 864, T, T),
 ]
-XF_BYTES = 8 * T
 
 
 def tile_moe_res_mlp_relu_kernel(
@@ -54,76 +53,51 @@ def tile_moe_res_mlp_relu_kernel(
             return psum.tile(shape, F32, name=name, tag=f"bank{b}", bufs=1)
 
         offsets = keep.tile([P, S // 16], U16, name="offsets")
-        w1s = [sb([P, PASSES * H], U8, f"w1s{e}") for e in range(E)]
+        w1s = [sb([P, PASSES * H], U8, "w1s0")]
         w2s = sb([P, E, N], U8, "w2s")
         w1 = {}
-        w2_first = sb([P, 2 * P], U8, "w2_first")
-        w2_rest = sb([P, 2 * (N - P)], U8, "w2_rest")
-        w2_other = sb([P, 2 * N], U8, "w2_other")
-
-        def w2(e, lo, hi):
-            if e == 1:
-                return w2_other[:, 2 * lo : 2 * hi].bitcast(E2M1)
-            if hi <= P:
-                return w2_first[:, 2 * lo : 2 * hi].bitcast(E2M1)
-            return w2_rest[:, 2 * (lo - P) : 2 * (hi - P)].bitcast(E2M1)
-
-        gate_four = sb([P, 4], F32, "gate_four")
-        gate_cols = sb([P, GROUPS - 1], F32, "gate_cols")
+        w2 = [sb([P, 2 * N], U8, f"w2_{e}") for e in range(E)]
         gates = sb([P, S], F32, "gates")
         ident = sb([P, P], F32, "ident")
-        stage = ctx.enter_context(tc.tile_pool(name="stage", bufs=1))
-        xf = [
-            stage.tile([P, 2 * (x[4] - x[2])], F32, name=f"xf{i}", align_bytes=64, offset=min(i, 7) * XF_BYTES + 8 * x[2])
-            for i, x in enumerate(LOADS)
-        ]
-        pairs_of = {(s, u): sb([P, T, 2], BF16, f"pairs{s}_{u}") for s in range(PASSES) for u in range(2)}
-        picked = {}
-        woven = {}
-        codes = {}
-        h = {}
-        h0 = [sb([P, H // 2], BF16, "h0_0"), sb([P, H // 2], BF16, "h0_1")]
-        hg = [turns.tile([P, P, PACK], BF16, name="hg0", align_bytes=64, offset=2048)]
-        hg.extend(sb([P, P, PACK], BF16, f"hg{g}") for g in range(1, GROUPS))
-        hq = [at(3072, [P, P], U32, "hq0")]
-        hq.extend(sb([P, P], U32, f"hq{g}") for g in range(1, GROUPS))
-        hs = [sb([P, P], U8, f"hs{g}") for g in range(GROUPS)]
-        y_slot = {}
+        xf = [sb([P, 2 * (x[5] - x[2])], F32, f"xf{i}") for i, x in enumerate(LOADS) if i < 6]
+        xf.append(at(24576, [P, 2 * T], F32, "xf6"))
+        xf.append(sb([P, 1024], F32, "xf7"))
+        xf.append(sb([P, 512], F32, "xf8"))
+        xf.append(sb([P, 512], F32, "xf9"))
+        gate_four = sb([P, 4], F32, "gate_four")
+        pairs_of = {(s, u): sb([P, T, 2], BF16, f"pairs{s}_{u}") for s in range(PASSES) for u in range(2) if 2 * s + u < 7}
+        pairs_of[PASSES - 1, 1] = at(10240, [P, T, 2], BF16, "pairs_last")
         back = [sb([P, T], F32, f"back{n}") for n in range(N_TILES)]
-        res = [sb([P, T], F32, f"res{n}") for n in range(N_TILES)]
 
+        nc.vector.memset(w1s[0][:].bitcast(I32), 0)
         nc.vector.memset(w2s[:].rearrange("p e i -> p (e i)").bitcast(I32), 0)
-        for e in range(E):
-            nc.vector.memset(w1s[e][:].bitcast(I32), 0)
         make_identity(nc, ident[:])
         for n in range(N_TILES):
             nc.gpsimd.memset(back[n][:], 0.0)
 
         def load_x(i):
-            s, u, t0, cut, t1 = LOADS[i]
+            s, u, t0, t1 = LOADS[i][0], LOADS[i][1], LOADS[i][2], LOADS[i][5]
             rows = xT[s * P * PACK : (s + 1) * P * PACK, t0:t1]
             nc.sync.dma_start(
                 out=xf[i][:].rearrange("p (e t) -> p e t", e=2),
                 in_=rows.rearrange("(p u e) t -> p u e t", u=2, e=2)[:, u, :, :],
             )
 
-        def load_w1(e, s0, s1):
-            tile = sb([P, s1 - s0, 2 * H], U8, f"w1_{e}_{s0}")
-            nc.sync.dma_start(
-                out=tile[:].bitcast(I32), in_=w1_words[e, s0:s1, :, :].bitcast(I32).rearrange("s p b -> p s b")
-            )
-            for s in range(s0, s1):
-                w1[e, s] = tile[:, s - s0, :]
-
-        def load_residual(n, lo, hi):
-            nc.sync.dma_start(out=res[n][:, lo:hi], in_=xr[n * P : (n + 1) * P, lo:hi])
-
-        def load_w1_scales(e):
+        def load_w1_scales(e, queue):
             rows = w1_scales[e].bitcast(I32).rearrange("s q i -> q s i")
             for r in range(4):
-                nc.sync.dma_start(
+                queue.dma_start(
                     out=w1s[e][r:P:32, :].bitcast(I32).rearrange("q (s i) -> q s i", s=PASSES), in_=rows[r:16:4, :, :]
                 )
+
+        def load_w1(e):
+            for s0 in range(0, PASSES, 2):
+                tile = sb([P, 2, 2 * H], U8, f"w1_{e}_{s0}")
+                nc.sync.dma_start(
+                    out=tile[:].bitcast(I32), in_=w1_words[e, s0 : s0 + 2, :, :].bitcast(I32).rearrange("s p b -> p s b")
+                )
+                for s in range(s0, s0 + 2):
+                    w1[e, s] = tile[:, s - s0, :]
 
         def load_w2_scales():
             rows = w2_scales[:, 0, :, :].bitcast(I32)
@@ -133,44 +107,40 @@ def tile_moe_res_mlp_relu_kernel(
                     in_=rows[:, r:16:4, :].rearrange("e q i -> q e i"),
                 )
 
+        def load_w2(e):
+            nc.sync.dma_start(out=w2[e][:].bitcast(I32), in_=w2_words[e, 0, :, :].bitcast(I32))
+
         load_x(0)
         nc.sync.dma_start(offsets[:], offs)
         nc.sync.dma_start(out=gate_four[:], in_=gate[0, :].rearrange("(p f) -> p f", f=4))
-        for i in range(1, len(LOADS) - 3):
-            load_x(i)
+        load_x(1)
+        load_x(2)
         load_w2_scales()
-        load_x(len(LOADS) - 3)
-        nc.sync.dma_start(out=w2_first[:].bitcast(I32), in_=w2_words[0, 0, :, 0 : 2 * P].bitcast(I32))
-        for i in range(len(LOADS) - 2, len(LOADS)):
+        load_x(3)
+        load_x(4)
+        load_w1_scales(0, nc.sync)
+        for i in range(5, 8):
             load_x(i)
-        load_w1_scales(0)
-        load_w1(0, 0, 2)
-        load_w1(0, 2, 4)
-        load_w1(1, 0, 2)
-        load_w1_scales(1)
-        nc.sync.dma_start(out=w2_rest[:].bitcast(I32), in_=w2_words[0, 0, :, 2 * P : 2 * N].bitcast(I32))
-        load_w1(1, 2, 4)
-        nc.sync.dma_start(out=w2_other[:].bitcast(I32), in_=w2_words[1, 0, :, :].bitcast(I32))
-        for n in range(N_TILES):
-            load_residual(n, 0, T)
+        load_w1(0)
+        for i in range(8, len(LOADS)):
+            load_x(i)
+        load_w1(1)
+        load_w2(0)
+        load_w2(1)
 
         spread_gate = bank(4, [P, 4, P], "spread_gate")
         for f in range(4):
             nc.tensor.transpose(spread_gate[:, f, :], gate_four[:, f : f + 1].to_broadcast([P, P]), ident[:])
         nc.scalar.copy(out=gates[:].rearrange("q (p f) -> q p f", f=4), in_=spread_gate[:].rearrange("q f p -> q p f"))
-        turned_gate = bank(5, [P, GROUPS - 1, P], "turned_gate")
-        for g in range(1, GROUPS):
-            nc.tensor.transpose(turned_gate[:, g - 1, :], gates[:, g * P : (g + 1) * P], ident[:])
-        nc.scalar.copy(out=gate_cols[:], in_=turned_gate[:, :, 0])
-
-        acc = {}
 
         def cast(i):
-            s, u, t0, cut, t1 = LOADS[i]
+            s, u, t0, cut0, cut1, t1 = LOADS[i]
             src = xf[i][:].rearrange("p (e t) -> p t e", e=2)
-            nc.scalar.activation(pairs_of[s, u][:, t0:cut, :], src[:, 0 : cut - t0, :], COPY)
-            if cut < t1:
-                nc.vector.tensor_copy(out=pairs_of[s, u][:, cut:t1, :], in_=src[:, cut - t0 : t1 - t0, :])
+            nc.scalar.activation(pairs_of[s, u][:, t0:cut0, :], src[:, 0 : cut0 - t0, :], COPY)
+            if cut0 < cut1:
+                nc.vector.tensor_copy(out=pairs_of[s, u][:, cut0:cut1, :], in_=src[:, cut0 - t0 : cut1 - t0, :])
+            if cut1 < t1:
+                nc.gpsimd.tensor_copy(out=pairs_of[s, u][:, cut1:t1, :], in_=src[:, cut1 - t0 : t1 - t0, :])
 
         def listed(lo, hi):
             return offsets[:, lo // 16 : hi // 16]
@@ -178,41 +148,63 @@ def tile_moe_res_mlp_relu_kernel(
         def window(s, u):
             return pairs_of[s, u][:].rearrange("p t e -> p (t e)").bitcast(U32)
 
-        def room(offset, n, name):
-            if offset is None:
-                return sb([P, n], U32, name)[:]
-            return stage.tile([P, n], U32, name=name, align_bytes=64, offset=offset)[:]
+        codes = {}
 
-        def weave(s, lo, hi, on_scalar, offset=None):
-            woven[s, lo] = room(offset, 2 * (hi - lo), f"woven{s}_{lo}")
-            dst = woven[s, lo].rearrange("p (n u) -> p n u", u=2)
-            src = picked[s][:, :, lo:hi].rearrange("p u n -> p n u")
-            if on_scalar:
-                nc.scalar.copy(out=dst, in_=src)
-            else:
-                nc.vector.tensor_copy(out=dst.bitcast(I32), in_=src.bitcast(I32))
-
-        def pick_plain(s, u, lo, hi):
-            if s not in picked:
-                picked[s] = sb([P, 2, S], U32, f"picked{s}")
-            nc.vector.tensor_copy(picked[s][:, u, lo:hi], window(s, u).indirect(listed(lo, hi)))
-
-        def pick_woven(s, u, lo, hi, offset=None):
-            if (s, lo) not in woven:
-                woven[s, lo] = room(offset, 2 * (hi - lo), f"woven{s}_{lo}")
-            nc.vector.tensor_copy(
-                woven[s, lo].rearrange("p (n u) -> p n u", u=2)[:, :, u], window(s, u).indirect(listed(lo, hi))
-            )
-
-        def quantise(s, lo, hi, offset=None):
-            words = room(offset, hi - lo, f"words{s}_{lo}")
+        def quantise(s, lo, hi, woven):
+            words = sb([P, hi - lo], U32, f"words{s}_{lo}")
             scales = sb([P, hi - lo], U8, f"scales{s}_{lo}")
-            nc.vector.quantize_mx(out=words.bitcast(E4M3), scales=scales[:], in_=woven[s, lo].bitcast(BF16))
+            nc.vector.quantize_mx(out=words[:].bitcast(E4M3), scales=scales[:], in_=woven.bitcast(BF16))
             for g in range(lo // P, hi // P):
                 cols = slice(g * P - lo, (g + 1) * P - lo)
                 codes[s, g] = (words[:, cols], scales[:, cols])
 
-        def first(s, g, start, stop):
+        last = PASSES - 1
+        for s in range(last):
+            picked = sb([P, 2, S], U32, f"picked{s}")
+            for u in range(2):
+                cast(2 * s + u)
+                nc.vector.tensor_copy(picked[:, u, :], window(s, u).indirect(listed(0, S)))
+            woven = sb([P, 2 * S], U32, f"woven{s}")
+            nc.vector.tensor_copy(
+                out=woven[:].rearrange("p (n u) -> p n u", u=2).bitcast(I32),
+                in_=picked[:].rearrange("p u n -> p n u").bitcast(I32),
+            )
+            quantise(s, 0, S, woven[:])
+
+        cuts = [(0, P), (P, C), (C, S)]
+        final = [at(4096, [P, 2 * P], U32, "final0")[:], sb([P, 2 * P], U32, "final1")[:], sb([P, 2 * C], U32, "final2")[:]]
+
+        def pick(u, j):
+            lo, hi = cuts[j]
+            nc.vector.tensor_copy(
+                final[j].rearrange("p (n u) -> p n u", u=2)[:, :, u], window(last, u).indirect(listed(lo, hi))
+            )
+
+        cast(2 * last)
+        for j in range(len(cuts)):
+            pick(0, j)
+        w1s.append(at(24576, [P, PASSES * H], U8, "w1s1"))
+        load_w1_scales(1, nc.scalar)
+        for i in range(2 * last + 1, len(LOADS)):
+            cast(i)
+        pick(1, 0)
+        pick(1, 1)
+        quantise(last, 0, P, final[0])
+        quantise(last, P, C, final[1])
+        late = at(4096, [P, C], U32, "late")
+        nc.vector.tensor_copy(late[:], window(last, 1).indirect(listed(C, S)))
+        nc.vector.tensor_copy(
+            out=final[2].rearrange("p (n u) -> p n u", u=2)[:, :, 1].bitcast(I32), in_=late[:].bitcast(I32)
+        )
+        quantise(last, C, S, final[2])
+
+        res = [at(offset, [P, T], F32, f"res{n}") for n, offset in enumerate((12288, 8192, 4096))]
+        for n in (1, 0, 2):
+            nc.sync.dma_start(out=res[n][:], in_=xr[n * P : (n + 1) * P, :])
+
+        acc = {}
+
+        def first(s, g):
             e = g // (C // P)
             nc.tensor.matmul_mx(
                 out=acc[g][:],
@@ -220,187 +212,92 @@ def tile_moe_res_mlp_relu_kernel(
                 lhsT_scale=codes[s, g][1],
                 rhs=w1[e, s].bitcast(E2M1),
                 rhs_scale=w1s[e][:, s * H : (s + 1) * H],
-                start=start,
-                stop=stop,
+                start=s == 0,
+                stop=s == last,
             )
 
-        last = PASSES - 1
-        spare = 8 * XF_BYTES
-        for s in range(last - 1):
-            cast(2 * s)
-            pick_plain(s, 0, 0, S)
-            cast(2 * s + 1)
-            for lo in (0, C):
-                pick_plain(s, 1, lo, lo + C)
-            for lo in (0, C):
-                weave(s, lo, lo + C, False)
-            for lo in (0, C):
-                quantise(s, lo, lo + C)
-        cast(2 * last - 2)
-        pick_plain(last - 1, 0, 0, S)
-        cast(2 * last - 1)
-        pick_plain(last - 1, 1, 0, C)
-        cast(2 * last)
-        weave(last - 1, 0, C, False, 2 * last * XF_BYTES)
-        pick_woven(last, 0, 0, P, spare)
-        pick_woven(last, 0, P, C, spare + 4096)
-        for i in range(2 * last + 1, len(LOADS)):
-            cast(i)
-        quantise(last - 1, 0, C, 8 * XF_BYTES - 1024)
-        pick_woven(last, 1, 0, P)
-        pick_woven(last, 1, P, C)
-        quantise(last, 0, P)
-        quantise(last, P, C)
-        late = stage.tile([P, 2, C], U32, name="late", align_bytes=64, offset=spare)
-        nc.vector.tensor_copy(late[:, 1, :], window(last - 1, 1).indirect(listed(C, S)))
-        nc.scalar.copy(out=late[:, 0, :], in_=picked[last - 1][:, 0, C:S])
-        woven[last - 1, C] = room(None, 2 * C, "woven_late")
-        nc.scalar.copy(
-            out=woven[last - 1, C].rearrange("p (n u) -> p n u", u=2), in_=late[:].rearrange("p u n -> p n u")
-        )
-        pick_woven(last, 0, C, S, spare + 4096)
-        pick_woven(last, 1, C, S)
-        quantise(last - 1, C, S)
-        quantise(last, C, S)
+        h = {}
+        hq = [sb([P, C], U32, f"hq{e}") for e in range(E)]
+        hs = [sb([P, C], U8, f"hs{e}") for e in range(E)]
 
         def activate(g):
-            if g == 0:
-                for w in range(2):
-                    sums = acc[0][:].rearrange("p (r w e) -> p w r e", w=2, e=2)[:, w, :, :]
-                    nc.scalar.activation(h0[w][:].rearrange("p (r e) -> p r e", e=2), sums, RELU)
-                return
-            h[g] = sb([P, H], BF16, "h1") if g == 1 else at(1024 + 1024 * g, [P, H], BF16, f"h{g}")
+            h[g] = sb([P, H], BF16, f"h{g}")
             nc.scalar.activation(
                 h[g][:].rearrange("p (w r e) -> p w r e", w=2, e=2),
                 acc[g][:].rearrange("p (r w e) -> p w r e", w=2, e=2),
                 RELU,
             )
 
-        def turn(g, b):
-            turned = bank(b, [P, 2, P], f"turned{g}")
+        def turn(g):
+            turned = bank(4 + g % 2, [P, 2, P], f"turned{g}")
             for w in range(2):
-                pairs = h0[w][:].bitcast(F32) if g == 0 else h[g][:].bitcast(F32)[:, w * P : (w + 1) * P]
-                nc.tensor.transpose(turned[:, w, :], pairs, ident[:])
-            dst = hg[g][:].rearrange("p r j -> p (r j)").bitcast(F32)
-            nc.scalar.copy(out=dst.rearrange("p (r w) -> p r w", w=2), in_=turned[:].rearrange("p w r -> p r w"))
+                nc.tensor.transpose(turned[:, w, :], h[g][:].bitcast(F32)[:, w * P : (w + 1) * P], ident[:])
+            hg = sb([P, P, 2], F32, f"hg{g}")
+            nc.scalar.copy(out=hg[:], in_=turned[:].rearrange("p w r -> p r w"))
+            e, cols = g // 2, slice(g % 2 * P, (g % 2 + 1) * P)
             nc.vector.quantize_mx(
-                out=hq[g][:].bitcast(E4M3), scales=hs[g][:], in_=hg[g][:].rearrange("p r j -> p (r j)")
+                out=hq[e][:, cols].bitcast(E4M3),
+                scales=hs[e][:, cols],
+                in_=hg[:].rearrange("p r w -> p (r w)").bitcast(BF16),
             )
 
-        def second(g, n, dst):
-            e = g // (C // P)
+        def second(e, n, lo, hi, dst):
             nc.tensor.matmul_mx(
                 out=dst,
-                lhsT=w2(e, P * n, P * (n + 1)),
+                lhsT=w2[e][:, 2 * P * n : 2 * P * (n + 1)].bitcast(E2M1),
                 lhsT_scale=w2s[:, e, n * P : (n + 1) * P],
-                rhs=hq[g][:].bitcast(E4M3),
-                rhs_scale=hs[g][:],
+                rhs=hq[e][:, lo:hi].bitcast(E4M3),
+                rhs_scale=hs[e][:, lo:hi],
                 start=True,
                 stop=True,
             )
 
-        def products(b, pairs):
-            y = bank(b, [P, len(pairs), P], "y%d_%d" % pairs[0])
-            for i, (g, n) in enumerate(pairs):
-                second(g, n, y[:, i, :])
-            return y
+        for g in range(GROUPS):
+            acc[g] = bank(g, [P, H], f"acc{g}")
 
-        def leave(y, name, offset=None):
-            shape = [P, y.shape[1], P]
-            y_rows = sb(shape, F32, name) if offset is None else at(offset, shape, F32, name)
-            nc.scalar.copy(out=y_rows[:], in_=y)
-            return y_rows
+        def passes(e):
+            for s in range(PASSES):
+                first(s, 2 * e)
+                first(s, 2 * e + 1)
 
-        def scatter(n, lo, hi, y_rows):
-            nc.vector.tensor_tensor(back[n][:].indirect(listed(lo, hi)), y_rows, gates[:, lo:hi], MULT)
+        passes(0)
+        def result(n, lo, hi, sums, offset=None):
+            e = lo // C
+            second(e, n, lo - e * C, hi - e * C, sums)
+            name = f"gated{n}_{lo}"
+            gated = sb([P, hi - lo], F32, name) if offset is None else at(offset, [P, hi - lo], F32, name)
+            nc.vector.tensor_tensor(gated[:], sums, gates[:, lo:hi], MULT)
+            if n == 1:
+                nc.vector.tensor_copy(back[n][:].indirect(listed(lo, hi)), gated[:])
+            else:
+                nc.scalar.activation(back[n][:].indirect(listed(lo, hi)), gated[:], COPY)
 
-        def by_slot(g, n0, b):
-            e = g // (C // P)
-            width = N - n0 * P
-            y = bank(b, [P, width], f"y_slot{g}")
-            nc.tensor.matmul_mx(
-                out=y[:],
-                lhsT=hq[g][:].bitcast(E4M3),
-                lhsT_scale=hs[g][:],
-                rhs=w2(e, n0 * P, N),
-                rhs_scale=w2s[:, e, n0 * P : N],
-                start=True,
-                stop=True,
-            )
-            gated = sb([P, width], F32, f"gated{g}")
-            nc.scalar.activation(gated[:], y[:], COPY, scale=gate_cols[:, g - 1 : g])
-            for n in range(n0, N_TILES):
-                y_slot[g, n] = gated[:, (n - n0) * P : (n - n0 + 1) * P]
-
-        def rest_rows(n, g0, b):
-            y = bank(b, [P, GROUPS - g0, P], f"y_back{n}")
-            for g in range(g0, GROUPS):
-                nc.tensor.transpose(y[:, g - g0, :], y_slot[g, n], ident[:])
-            y_gated = sb([P, S - g0 * P], F32, f"y_gated{n}")
-            nc.scalar.copy(out=y_gated[:], in_=y[:].rearrange("p g r -> p (g r)"))
-            nc.vector.tensor_copy(back[n][:].indirect(listed(g0 * P, S)), y_gated[:])
-
-        def add_turned(n, lo, hi, b_there, b_back):
-            chunks = (hi - lo) // P
-            there = bank(b_there, [P, chunks, P], f"sum_there{n}")
-            for c in range(chunks):
-                cols = slice(lo + c * P, lo + (c + 1) * P)
-                nc.tensor.matmul(there[:, c, :], res[n][:, cols], ident[:], start=True, stop=False, is_transpose=True)
-                nc.tensor.matmul(there[:, c, :], back[n][:, cols], ident[:], start=False, stop=True, is_transpose=True)
-            by_token = sb([P, chunks, P], F32, f"sum_by_token{n}")
-            nc.scalar.copy(out=by_token[:], in_=there[:])
-            again = bank(b_back, [P, chunks * P], f"sum_again{n}")
-            for c in range(chunks):
-                nc.tensor.transpose(again[:, c * P : (c + 1) * P], by_token[:, c, :], ident[:])
-            nc.scalar.copy(out=res[n][:, lo:hi], in_=again[:])
-            nc.scalar.dma_start(out=out[n * P : (n + 1) * P, lo:hi], in_=res[n][:, lo:hi])
-
-        def passes(g, order):
-            for s in order:
-                first(s, g, s == 0, s == last)
-
-        def add(engine, n, lo, hi):
-            engine.tensor_tensor(res[n][:, lo:hi], back[n][:, lo:hi], res[n][:, lo:hi], ADD)
-            nc.sync.dma_start(out=out[n * P : (n + 1) * P, lo:hi], in_=res[n][:, lo:hi])
-
-        acc[0] = bank(0, [P, H], "acc0")
-        acc[1] = bank(1, [P, H], "acc1")
-        acc[3] = bank(2, [P, H], "acc3")
-        for s in range(PASSES):
-            passes(0, [s])
-            passes(1, [s])
         activate(0)
-        turn(0, 4)
         activate(1)
-        turn(1, 5)
-        y00 = leave(products(0, [(0, 0)])[:], "y00")
-        scatter(0, 0, P, y00[:, 0, :])
-        y0 = products(3, [(0, 1), (0, 2)])
-        y01 = leave(y0[:, 0:1, :], "y01")
-        scatter(1, 0, P, y01[:, 0, :])
-        y1 = leave(products(4, [(1, 0), (1, 1)])[:], "y1")
-        scatter(0, P, C, y1[:, 0, :])
-        scatter(1, P, C, y1[:, 1, :])
-        acc[2] = bank(1, [P, H], "acc2")
-        passes(2, range(PASSES))
+        turn(0)
+        turn(1)
+        result(1, 0, P, bank(6, [P, P], "y1_0")[:])
+        passes(1)
         activate(2)
-        passes(3, range(PASSES))
         activate(3)
-        turn(2, 6)
-        turn(3, 5)
-        y02 = leave(y0[:, 1:2, :], "y02", 4096)
-        scatter(2, 0, P, y02[:, 0, :])
-        by_slot(1, 2, 2)
-        y23 = leave(products(0, [(2, 0), (3, 0)])[:], "y23")
-        scatter(0, C, S, y23[:].rearrange("p g r -> p (g r)"))
-        by_slot(2, 1, 1)
-        by_slot(3, 1, 2)
-        add(nc.gpsimd, 0, 0, 512)
-        rest_rows(1, 2, 3)
-        add(nc.gpsimd, 1, 0, 384)
-        add(nc.gpsimd, 1, 384, 768)
-        rest_rows(2, 1, 7)
-        add_turned(0, 512, T, 3, 7)
-        add_turned(1, 768, T, 0, 1)
+        turn(2)
+        turn(3)
+        both = bank(3, [P, 2, C], "y02_0")
+        result(0, 0, C, both[:, 0, :])
+        result(2, 0, C, both[:, 1, :])
+        result(1, P, C, bank(5, [P, P], "y1_1")[:])
+        result(0, C, S, bank(7, [P, C], "y0_2")[:])
+        result(2, C, S, bank(0, [P, C], "y2_2")[:])
+        result(1, C, S, bank(1, [P, C], "y1_2")[:], 0)
+
+        def add(engine, n, lo, hi, dst):
+            engine.tensor_tensor(dst, back[n][:, lo:hi], res[n][:, lo:hi], ADD)
+            nc.sync.dma_start(out=out[n * P : (n + 1) * P, lo:hi], in_=dst)
+
+        sums = sb([P, T], F32, "sums")
+        for lo in range(0, T, 512):
+            add(nc.vector, 1, lo, lo + 512, sums[:, lo : lo + 512])
+        add(nc.gpsimd, 0, 0, 512, back[1][:, 0:512])
+        add(nc.vector, 0, 512, T, at(0, [P, 512], F32, "sums0")[:])
         for lo in range(0, T, 256):
-            add(nc.vector, 2, lo, lo + 256)
+            add(nc.vector, 2, lo, lo + 256, res[1][:, lo : lo + 256])

@@ -30,7 +30,7 @@ ADD = mybir.AluOpType.add
 LOADS = [
     (0, 0, 0, 384, T, T), (0, 1, 0, 640, T, T), (1, 0, 0, 768, 768, T), (1, 1, 0, 768, 768, T),
     (2, 0, 0, 768, 768, T), (2, 1, 0, 768, 768, T), (3, 0, 0, 768, 768, T),
-    (3, 1, 0, 320, 320, 512), (3, 1, 512, 672, 672, 768), (3, 1, 768, 864, T, T),
+    (3, 1, 0, 320, 320, 512), (3, 1, 512, 672, 672, 768), (3, 1, 768, 768, T, T),
 ]
 
 
@@ -53,23 +53,20 @@ def tile_moe_res_mlp_relu_kernel(
             return psum.tile(shape, F32, name=name, tag=f"bank{b}", bufs=1)
 
         offsets = keep.tile([P, S // 16], U16, name="offsets")
-        w1s = [sb([P, PASSES * H], U8, "w1s0")]
+        w1s = [sb([P, PASSES * H], U8, f"w1s{e}") for e in range(E)]
         w2s = sb([P, E, N], U8, "w2s")
         w1 = {}
         w2 = [sb([P, 2 * N], U8, f"w2_{e}") for e in range(E)]
         gates = sb([P, S], F32, "gates")
         ident = sb([P, P], F32, "ident")
-        xf = [sb([P, 2 * (x[5] - x[2])], F32, f"xf{i}") for i, x in enumerate(LOADS) if i < 6]
-        xf.append(at(24576, [P, 2 * T], F32, "xf6"))
-        xf.append(sb([P, 1024], F32, "xf7"))
-        xf.append(sb([P, 512], F32, "xf8"))
-        xf.append(sb([P, 512], F32, "xf9"))
+        xf = [sb([P, 2, T], F32, f"xf{i}") for i in range(2 * PASSES)]
         gate_four = sb([P, 4], F32, "gate_four")
         pairs_of = {(s, u): sb([P, T, 2], BF16, f"pairs{s}_{u}") for s in range(PASSES) for u in range(2) if 2 * s + u < 7}
         pairs_of[PASSES - 1, 1] = at(10240, [P, T, 2], BF16, "pairs_last")
         back = [sb([P, T], F32, f"back{n}") for n in range(N_TILES)]
 
-        nc.vector.memset(w1s[0][:].bitcast(I32), 0)
+        for e in range(E):
+            nc.vector.memset(w1s[e][:].bitcast(I32), 0)
         nc.vector.memset(w2s[:].rearrange("p e i -> p (e i)").bitcast(I32), 0)
         make_identity(nc, ident[:])
         for n in range(N_TILES):
@@ -79,7 +76,7 @@ def tile_moe_res_mlp_relu_kernel(
             s, u, t0, t1 = LOADS[i][0], LOADS[i][1], LOADS[i][2], LOADS[i][5]
             rows = xT[s * P * PACK : (s + 1) * P * PACK, t0:t1]
             nc.sync.dma_start(
-                out=xf[i][:].rearrange("p (e t) -> p e t", e=2),
+                out=xf[2 * s + u][:, :, t0:t1],
                 in_=rows.rearrange("(p u e) t -> p u e t", u=2, e=2)[:, u, :, :],
             )
 
@@ -90,8 +87,8 @@ def tile_moe_res_mlp_relu_kernel(
                     out=w1s[e][r:P:32, :].bitcast(I32).rearrange("q (s i) -> q s i", s=PASSES), in_=rows[r:16:4, :, :]
                 )
 
-        def load_w1(e):
-            for s0 in range(0, PASSES, 2):
+        def load_w1(e, starts):
+            for s0 in starts:
                 tile = sb([P, 2, 2 * H], U8, f"w1_{e}_{s0}")
                 nc.sync.dma_start(
                     out=tile[:].bitcast(I32), in_=w1_words[e, s0 : s0 + 2, :, :].bitcast(I32).rearrange("s p b -> p s b")
@@ -119,12 +116,14 @@ def tile_moe_res_mlp_relu_kernel(
         load_x(3)
         load_x(4)
         load_w1_scales(0, nc.sync)
-        for i in range(5, 8):
+        load_x(5)
+        load_w1_scales(1, nc.sync)
+        load_x(6)
+        load_w1(0, [0])
+        for i in range(7, len(LOADS)):
             load_x(i)
-        load_w1(0)
-        for i in range(8, len(LOADS)):
-            load_x(i)
-        load_w1(1)
+        load_w1(0, [2])
+        load_w1(1, [0, 2])
         load_w2(0)
         load_w2(1)
 
@@ -135,12 +134,13 @@ def tile_moe_res_mlp_relu_kernel(
 
         def cast(i):
             s, u, t0, cut0, cut1, t1 = LOADS[i]
-            src = xf[i][:].rearrange("p (e t) -> p t e", e=2)
-            nc.scalar.activation(pairs_of[s, u][:, t0:cut0, :], src[:, 0 : cut0 - t0, :], COPY)
+            src = xf[2 * s + u][:].rearrange("p e t -> p t e")
+            if t0 < cut0:
+                nc.scalar.activation(pairs_of[s, u][:, t0:cut0, :], src[:, t0:cut0, :], COPY)
             if cut0 < cut1:
-                nc.vector.tensor_copy(out=pairs_of[s, u][:, cut0:cut1, :], in_=src[:, cut0 - t0 : cut1 - t0, :])
+                nc.vector.tensor_copy(out=pairs_of[s, u][:, cut0:cut1, :], in_=src[:, cut0:cut1, :])
             if cut1 < t1:
-                nc.gpsimd.tensor_copy(out=pairs_of[s, u][:, cut1:t1, :], in_=src[:, cut1 - t0 : t1 - t0, :])
+                nc.gpsimd.tensor_copy(out=pairs_of[s, u][:, cut1:t1, :], in_=src[:, cut1:t1, :])
 
         def listed(lo, hi):
             return offsets[:, lo // 16 : hi // 16]
@@ -171,8 +171,8 @@ def tile_moe_res_mlp_relu_kernel(
             )
             quantise(s, 0, S, woven[:])
 
-        cuts = [(0, P), (P, C), (C, S)]
-        final = [at(4096, [P, 2 * P], U32, "final0")[:], sb([P, 2 * P], U32, "final1")[:], sb([P, 2 * C], U32, "final2")[:]]
+        cuts = [(0, P), (P, C)]
+        final = [at(4096, [P, 2 * P], U32, "final0")[:], sb([P, 2 * P], U32, "final1")[:]]
 
         def pick(u, j):
             lo, hi = cuts[j]
@@ -183,20 +183,21 @@ def tile_moe_res_mlp_relu_kernel(
         cast(2 * last)
         for j in range(len(cuts)):
             pick(0, j)
-        w1s.append(at(24576, [P, PASSES * H], U8, "w1s1"))
-        load_w1_scales(1, nc.scalar)
         for i in range(2 * last + 1, len(LOADS)):
             cast(i)
         pick(1, 0)
         pick(1, 1)
         quantise(last, 0, P, final[0])
         quantise(last, P, C, final[1])
-        late = at(4096, [P, C], U32, "late")
-        nc.vector.tensor_copy(late[:], window(last, 1).indirect(listed(C, S)))
+        late = at(4096, [P, 2, C], U32, "late")
+        for u in range(2):
+            nc.vector.tensor_copy(late[:, u, :], window(last, u).indirect(listed(C, S)))
+        woven = sb([P, 2 * C], U32, "woven_late")
         nc.vector.tensor_copy(
-            out=final[2].rearrange("p (n u) -> p n u", u=2)[:, :, 1].bitcast(I32), in_=late[:].bitcast(I32)
+            out=woven[:].rearrange("p (n u) -> p n u", u=2).bitcast(I32),
+            in_=late[:].rearrange("p u n -> p n u").bitcast(I32),
         )
-        quantise(last, C, S, final[2])
+        quantise(last, C, S, woven[:])
 
         res = [at(offset, [P, T], F32, f"res{n}") for n, offset in enumerate((12288, 8192, 4096))]
         for n in (1, 0, 2):
@@ -217,28 +218,31 @@ def tile_moe_res_mlp_relu_kernel(
             )
 
         h = {}
+        hg = [sb([P, C, 2], F32, f"hg{e}") for e in range(E)]
         hq = [sb([P, C], U32, f"hq{e}") for e in range(E)]
         hs = [sb([P, C], U8, f"hs{e}") for e in range(E)]
 
         def activate(g):
             h[g] = sb([P, H], BF16, f"h{g}")
-            nc.scalar.activation(
-                h[g][:].rearrange("p (w r e) -> p w r e", w=2, e=2),
-                acc[g][:].rearrange("p (r w e) -> p w r e", w=2, e=2),
-                RELU,
-            )
+            dst = h[g][:].rearrange("p (w r e) -> p w r e", w=2, e=2)
+            src = acc[g][:].rearrange("p (r w e) -> p w r e", w=2, e=2)
+            nc.scalar.activation(dst, src, RELU)
 
         def turn(g):
             turned = bank(4 + g % 2, [P, 2, P], f"turned{g}")
             for w in range(2):
                 nc.tensor.transpose(turned[:, w, :], h[g][:].bitcast(F32)[:, w * P : (w + 1) * P], ident[:])
-            hg = sb([P, P, 2], F32, f"hg{g}")
-            nc.scalar.copy(out=hg[:], in_=turned[:].rearrange("p w r -> p r w"))
-            e, cols = g // 2, slice(g % 2 * P, (g % 2 + 1) * P)
+            dst = hg[g // 2][:, g % 2 * P : (g % 2 + 1) * P, :]
+            if g < 2:
+                nc.scalar.copy(out=dst, in_=turned[:].rearrange("p w r -> p r w"))
+            else:
+                nc.vector.tensor_copy(out=dst, in_=turned[:].rearrange("p w r -> p r w"))
+
+        def quantise_hidden(e, lo, hi):
             nc.vector.quantize_mx(
-                out=hq[e][:, cols].bitcast(E4M3),
-                scales=hs[e][:, cols],
-                in_=hg[:].rearrange("p r w -> p (r w)").bitcast(BF16),
+                out=hq[e][:, lo:hi].bitcast(E4M3),
+                scales=hs[e][:, lo:hi],
+                in_=hg[e][:, lo:hi, :].rearrange("p r w -> p (r w)").bitcast(BF16),
             )
 
         def second(e, n, lo, hi, dst):
@@ -261,34 +265,46 @@ def tile_moe_res_mlp_relu_kernel(
                 first(s, 2 * e + 1)
 
         passes(0)
-        def result(n, lo, hi, sums, offset=None):
+        def result(n, lo, hi, b, gated):
             e = lo // C
-            second(e, n, lo - e * C, hi - e * C, sums)
-            name = f"gated{n}_{lo}"
-            gated = sb([P, hi - lo], F32, name) if offset is None else at(offset, [P, hi - lo], F32, name)
-            nc.vector.tensor_tensor(gated[:], sums, gates[:, lo:hi], MULT)
-            if n == 1:
-                nc.vector.tensor_copy(back[n][:].indirect(listed(lo, hi)), gated[:])
-            else:
-                nc.scalar.activation(back[n][:].indirect(listed(lo, hi)), gated[:], COPY)
+            sums = bank(b, [P, hi - lo], f"y{n}_{lo}")
+            second(e, n, lo - e * C, hi - e * C, sums[:])
+            nc.vector.tensor_tensor(gated, sums[:], gates[:, lo:hi], MULT)
 
+        def scatter(n, lo, hi, gated):
+            if n == 1:
+                nc.vector.tensor_copy(back[n][:].indirect(listed(lo, hi)), gated)
+            else:
+                nc.scalar.activation(back[n][:].indirect(listed(lo, hi)), gated, COPY)
+
+        gated0 = sb([P, S], F32, "gated0")
+        gated2 = sb([P, S], F32, "gated2")
+        gated1 = [sb([P, P], F32, "gated1_0"), at(0, [P, S - P], F32, "gated1_1")]
         activate(0)
         activate(1)
         turn(0)
         turn(1)
-        result(1, 0, P, bank(6, [P, P], "y1_0")[:])
+        quantise_hidden(0, 0, P)
+        result(1, 0, P, 6, gated1[0][:])
+        quantise_hidden(0, P, C)
+        scatter(1, 0, P, gated1[0][:])
         passes(1)
         activate(2)
         activate(3)
+        result(0, 0, C, 2, gated0[:, 0:C])
+        scatter(0, 0, C, gated0[:, 0:C])
         turn(2)
+        result(2, 0, C, 3, gated2[:, 0:C])
+        scatter(2, 0, P, gated2[:, 0:P])
         turn(3)
-        both = bank(3, [P, 2, C], "y02_0")
-        result(0, 0, C, both[:, 0, :])
-        result(2, 0, C, both[:, 1, :])
-        result(1, P, C, bank(5, [P, P], "y1_1")[:])
-        result(0, C, S, bank(7, [P, C], "y0_2")[:])
-        result(2, C, S, bank(0, [P, C], "y2_2")[:])
-        result(1, C, S, bank(1, [P, C], "y1_2")[:], 0)
+        quantise_hidden(1, 0, C)
+        result(0, C, S, 0, gated0[:, C:S])
+        scatter(0, C, S, gated0[:, C:S])
+        result(2, C, S, 1, gated2[:, C:S])
+        scatter(2, P, S, gated2[:, P:S])
+        result(1, P, C, 0, gated1[1][:, 0:P])
+        result(1, C, S, 7, gated1[1][:, P:])
+        scatter(1, P, S, gated1[1][:])
 
         def add(engine, n, lo, hi, dst):
             engine.tensor_tensor(dst, back[n][:, lo:hi], res[n][:, lo:hi], ADD)
@@ -297,7 +313,7 @@ def tile_moe_res_mlp_relu_kernel(
         sums = sb([P, T], F32, "sums")
         for lo in range(0, T, 512):
             add(nc.vector, 1, lo, lo + 512, sums[:, lo : lo + 512])
-        add(nc.gpsimd, 0, 0, 512, back[1][:, 0:512])
-        add(nc.vector, 0, 512, T, at(0, [P, 512], F32, "sums0")[:])
+        for lo in range(0, T, 256):
+            add(nc.gpsimd, 0, lo, lo + 256, back[0][:, lo : lo + 256])
         for lo in range(0, T, 256):
             add(nc.vector, 2, lo, lo + 256, res[1][:, lo : lo + 256])

@@ -29,7 +29,7 @@ ADD = mybir.AluOpType.add
 
 LOADS = [
     (0, 0, 0, 384, T, T), (0, 1, 0, 640, T, T), (1, 0, 0, 768, 768, T), (1, 1, 0, 768, 768, T),
-    (2, 0, 0, 768, 768, T), (2, 1, 0, 768, 768, T), (3, 0, 0, 768, 768, T),
+    (2, 0, 0, 768, 768, T), (2, 1, 0, 640, 640, T), (3, 0, 0, 640, 640, T),
     (3, 1, 0, 320, 320, 512), (3, 1, 512, 672, 672, 768), (3, 1, 768, 768, T, T),
 ]
 
@@ -311,9 +311,9 @@ def tile_moe_res_mlp_relu_kernel(
             nc.sync.dma_start(out=out[n * P : (n + 1) * P, lo:hi], in_=dst)
 
         sums = sb([P, T], F32, "sums")
+        add(nc.gpsimd, 0, 0, 512, back[0][:, 0:512])
         for lo in range(0, T, 512):
             add(nc.vector, 1, lo, lo + 512, sums[:, lo : lo + 512])
-        for lo in range(0, T, 256):
-            add(nc.gpsimd, 0, lo, lo + 256, back[0][:, lo : lo + 256])
+        add(nc.vector, 0, 512, T, back[1][:, 0:512])
         for lo in range(0, T, 256):
             add(nc.vector, 2, lo, lo + 256, res[1][:, lo : lo + 256])

@@ -112,12 +112,12 @@ def tile_moe_res_mlp_relu_kernel(
         nc.sync.dma_start(out=gate_four[:], in_=gate[0, :].rearrange("(p f) -> p f", f=4))
         load_x(1)
         load_x(2)
-        load_w2_scales()
+        load_w1_scales(0, nc.sync)
         load_x(3)
         load_x(4)
-        load_w1_scales(0, nc.sync)
-        load_x(5)
         load_w1_scales(1, nc.sync)
+        load_x(5)
+        load_w2_scales()
         load_x(6)
         load_w1(0, [0])
         for i in range(7, len(LOADS)):
@@ -265,11 +265,20 @@ def tile_moe_res_mlp_relu_kernel(
                 first(s, 2 * e + 1)
 
         passes(0)
+        def results(b, parts):
+            sums = bank(b, [P, sum(hi - lo for n, lo, hi, gated in parts)], "y%d_%d" % parts[0][:2])
+            at_col = 0
+            for n, lo, hi, gated in parts:
+                e = lo // C
+                second(e, n, lo - e * C, hi - e * C, sums[:, at_col : at_col + hi - lo])
+                at_col = at_col + hi - lo
+            at_col = 0
+            for n, lo, hi, gated in parts:
+                nc.vector.tensor_tensor(gated, sums[:, at_col : at_col + hi - lo], gates[:, lo:hi], MULT)
+                at_col = at_col + hi - lo
+
         def result(n, lo, hi, b, gated):
-            e = lo // C
-            sums = bank(b, [P, hi - lo], f"y{n}_{lo}")
-            second(e, n, lo - e * C, hi - e * C, sums[:])
-            nc.vector.tensor_tensor(gated, sums[:], gates[:, lo:hi], MULT)
+            results(b, [(n, lo, hi, gated)])
 
         def scatter(n, lo, hi, gated):
             if n == 1:
@@ -294,15 +303,14 @@ def tile_moe_res_mlp_relu_kernel(
         result(0, 0, C, 2, gated0[:, 0:C])
         scatter(0, 0, C, gated0[:, 0:C])
         turn(2)
-        result(2, 0, C, 3, gated2[:, 0:C])
-        scatter(2, 0, P, gated2[:, 0:P])
         turn(3)
         quantise_hidden(1, 0, C)
+        results(5, [(2, 0, C, gated2[:, 0:C]), (1, P, C, gated1[1][:, 0:P])])
+        scatter(2, 0, P, gated2[:, 0:P])
         result(0, C, S, 0, gated0[:, C:S])
         scatter(0, C, S, gated0[:, C:S])
         result(2, C, S, 1, gated2[:, C:S])
         scatter(2, P, S, gated2[:, P:S])
-        result(1, P, C, 0, gated1[1][:, 0:P])
         result(1, C, S, 7, gated1[1][:, P:])
         scatter(1, P, S, gated1[1][:])
 

@@ -28,9 +28,9 @@ MULT = mybir.AluOpType.mult
 ADD = mybir.AluOpType.add
 
 LOADS = [
-    (0, 0, 0, 384, T, T), (0, 1, 0, 640, T, T), (1, 0, 0, 768, 768, T), (1, 1, 0, 768, 768, T),
-    (2, 0, 0, 768, 768, T), (2, 1, 0, 640, 640, T), (3, 0, 0, 640, 640, T),
-    (3, 1, 0, 320, 320, 512), (3, 1, 512, 672, 672, 768), (3, 1, 768, 768, T, T),
+    (0, 0, 0, 384, T, T), (0, 1, 0, 640, T, T), (1, 0, 0, 768, 768, T), (1, 1, 0, 640, 640, T),
+    (2, 0, 0, 768, 768, T), (2, 1, 0, 576, 576, T), (3, 0, 0, 832, 832, T),
+    (3, 1, 0, 256, 256, 512), (3, 1, 512, 640, 640, 768), (3, 1, 768, 768, T, T),
 ]
 
 
@@ -165,11 +165,13 @@ def tile_moe_res_mlp_relu_kernel(
                 cast(2 * s + u)
                 nc.vector.tensor_copy(picked[:, u, :], window(s, u).indirect(listed(0, S)))
             woven = sb([P, 2 * S], U32, f"woven{s}")
-            nc.vector.tensor_copy(
-                out=woven[:].rearrange("p (n u) -> p n u", u=2).bitcast(I32),
-                in_=picked[:].rearrange("p u n -> p n u").bitcast(I32),
-            )
-            quantise(s, 0, S, woven[:])
+            for lo in (0, C):
+                nc.vector.tensor_copy(
+                    out=woven[:, 2 * lo : 2 * (lo + C)].rearrange("p (n u) -> p n u", u=2).bitcast(I32),
+                    in_=picked[:, :, lo : lo + C].rearrange("p u n -> p n u").bitcast(I32),
+                )
+            for lo in (0, C):
+                quantise(s, lo, lo + C, woven[:, 2 * lo : 2 * (lo + C)])
 
         cuts = [(0, P), (P, C)]
         final = [at(4096, [P, 2 * P], U32, "final0")[:], sb([P, 2 * P], U32, "final1")[:]]
@@ -323,5 +325,5 @@ def tile_moe_res_mlp_relu_kernel(
         for lo in range(0, T, 512):
             add(nc.vector, 1, lo, lo + 512, sums[:, lo : lo + 512])
         add(nc.vector, 0, 512, T, back[1][:, 0:512])
-        for lo in range(0, T, 256):
-            add(nc.vector, 2, lo, lo + 256, res[1][:, lo : lo + 256])
+        for lo, hi in ((0, 512), (512, 768), (768, T)):
+            add(nc.vector, 2, lo, hi, res[1][:, lo:hi])

@@ -28,9 +28,9 @@ MULT = mybir.AluOpType.mult
 ADD = mybir.AluOpType.add
 
 LOADS = [
-    (0, 0, 0, 384, T, T), (0, 1, 0, 640, T, T), (1, 0, 0, 768, 768, T), (1, 1, 0, 640, 640, T),
-    (2, 0, 0, 768, 768, T), (2, 1, 0, 576, 576, T), (3, 0, 0, 832, 832, T),
-    (3, 1, 0, 256, 256, 512), (3, 1, 512, 640, 640, 768), (3, 1, 768, 768, T, T),
+    (0, 0, 0, 448, T, T), (0, 1, 0, 640, 640, T), (1, 0, 0, 768, 768, T), (1, 1, 0, 640, 640, T),
+    (2, 0, 0, 768, 768, T), (2, 1, 0, 624, 624, T), (3, 0, 0, 832, 832, T),
+    (3, 1, 0, 256, 256, 512), (3, 1, 512, 640, 640, 768), (3, 1, 768, 880, T, T),
 ]
 
 
@@ -161,9 +161,11 @@ def tile_moe_res_mlp_relu_kernel(
         last = PASSES - 1
         for s in range(last):
             picked = sb([P, 2, S], U32, f"picked{s}")
-            for u in range(2):
-                cast(2 * s + u)
-                nc.vector.tensor_copy(picked[:, u, :], window(s, u).indirect(listed(0, S)))
+            cast(2 * s)
+            nc.vector.tensor_copy(picked[:, 0, :], window(s, 0).indirect(listed(0, S)))
+            cast(2 * s + 1)
+            for lo in (0, C):
+                nc.vector.tensor_copy(picked[:, 1, lo : lo + C], window(s, 1).indirect(listed(lo, lo + C)))
             woven = sb([P, 2 * S], U32, f"woven{s}")
             for lo in (0, C):
                 nc.vector.tensor_copy(
@@ -192,14 +194,17 @@ def tile_moe_res_mlp_relu_kernel(
         quantise(last, 0, P, final[0])
         quantise(last, P, C, final[1])
         late = at(4096, [P, 2, C], U32, "late")
-        for u in range(2):
-            nc.vector.tensor_copy(late[:, u, :], window(last, u).indirect(listed(C, S)))
+        nc.vector.tensor_copy(late[:, 0, :], window(last, 0).indirect(listed(C, S)))
+        for lo in (0, P):
+            nc.vector.tensor_copy(late[:, 1, lo : lo + P], window(last, 1).indirect(listed(C + lo, C + lo + P)))
         woven = sb([P, 2 * C], U32, "woven_late")
-        nc.vector.tensor_copy(
-            out=woven[:].rearrange("p (n u) -> p n u", u=2).bitcast(I32),
-            in_=late[:].rearrange("p u n -> p n u").bitcast(I32),
-        )
-        quantise(last, C, S, woven[:])
+        for lo in (0, P):
+            nc.vector.tensor_copy(
+                out=woven[:, 2 * lo : 2 * (lo + P)].rearrange("p (n u) -> p n u", u=2).bitcast(I32),
+                in_=late[:, :, lo : lo + P].rearrange("p u n -> p n u").bitcast(I32),
+            )
+        for lo in (0, P):
+            quantise(last, C + lo, C + lo + P, woven[:, 2 * lo : 2 * (lo + P)])
 
         res = [at(offset, [P, T], F32, f"res{n}") for n, offset in enumerate((12288, 8192, 4096))]
         for n in (1, 0, 2):
@@ -311,9 +316,9 @@ def tile_moe_res_mlp_relu_kernel(
         scatter(2, 0, P, gated2[:, 0:P])
         result(0, C, S, 0, gated0[:, C:S])
         scatter(0, C, S, gated0[:, C:S])
+        result(1, C, S, 7, gated1[1][:, P:])
         result(2, C, S, 1, gated2[:, C:S])
         scatter(2, P, S, gated2[:, P:S])
-        result(1, C, S, 7, gated1[1][:, P:])
         scatter(1, P, S, gated1[1][:])
 
         def add(engine, n, lo, hi, dst):

@@ -115,13 +115,13 @@ def tile_moe_res_mlp_relu_kernel(
         load_w1_scales(0, nc.sync)
         load_x(3)
         load_x(4)
-        load_w1_scales(1, nc.sync)
         load_x(5)
         load_w2_scales()
         load_x(6)
         load_w1(0, [0])
         for i in range(7, len(LOADS)):
             load_x(i)
+        load_w1_scales(1, nc.sync)
         load_w1(0, [2])
         load_w1(1, [0, 2])
         load_w2(0)

from contextlib import ExitStack

import concourse.mybir as mybir
from concourse.masks import make_identity

K, T, E, C, H, N = 2048, 1024, 2, 256, 512, 384
P = 128
PACK = 4
PASSES = K // (P * PACK)
S = E * C
GROUPS = S // P
N_TILES = N // P

FLOPS = 2 * S * (K * H + H * N)
BYTES = 4 * (K * T + 2 * N * T + S) + E * (K * H + H * N) // 2 + E * (K * H + H * N) // 32 + 2 * P * S // 16

F32 = mybir.dt.float32
BF16 = mybir.dt.bfloat16
U32 = mybir.dt.uint32
I32 = mybir.dt.int32
U16 = mybir.dt.uint16
U8 = mybir.dt.uint8
E4M3 = mybir.dt.float8_e4m3fn_x4
E2M1 = mybir.dt.float4_e2m1fn_x4
COPY = mybir.ActivationFunctionType.Copy
RELU = mybir.ActivationFunctionType.Relu
MULT = mybir.AluOpType.mult
ADD = mybir.AluOpType.add

LOADS = [
    (0, 0, 0, 448, T, T), (0, 1, 0, 640, 640, T), (1, 0, 0, 768, 768, T), (1, 1, 0, 640, 640, T),
    (2, 0, 0, 768, 768, T), (2, 1, 0, 624, 624, T), (3, 0, 0, 832, 832, T),
    (3, 1, 0, 256, 256, 512), (3, 1, 512, 640, 640, 768), (3, 1, 768, 880, T, T),
]


def tile_moe_res_mlp_relu_kernel(
    tc, xT, xr, w1_words, w1_scales, w2_words, w2_scales, gate, offs, out
):
    nc = tc.nc
    with ExitStack() as ctx:
        keep = ctx.enter_context(tc.tile_pool(name="keep", bufs=1))
        turns = ctx.enter_context(tc.tile_pool(name="turns", bufs=1))
        psum = ctx.enter_context(tc.psum_pool(name="psum", bufs=1))

        def sb(shape, dtype, name):
            return keep.tile(shape, dtype, name=name, align_bytes=64)

        def at(offset, shape, dtype, name):
            return turns.tile(shape, dtype, name=name, align_bytes=64, offset=offset)

        def bank(b, shape, name):
            return psum.tile(shape, F32, name=name, tag=f"bank{b}", bufs=1)

        offsets = keep.tile([P, S // 16], U16, name="offsets")
        w1s = [sb([P, PASSES * H], U8, f"w1s{e}") for e in range(E)]
        w2s = sb([P, E, N], U8, "w2s")
        w1 = {}
        w2 = [sb([P, 2 * N], U8, f"w2_{e}") for e in range(E)]
        gates = sb([P, S], F32, "gates")
        ident = sb([P, P], F32, "ident")
        xf = [sb([P, 2, T], F32, f"xf{i}") for i in range(2 * PASSES)]
        gate_four = sb([P, 4], F32, "gate_four")
        pairs_of = {(s, u): sb([P, T, 2], BF16, f"pairs{s}_{u}") for s in range(PASSES) for u in range(2) if 2 * s + u < 7}
        pairs_of[PASSES - 1, 1] = at(10240, [P, T, 2], BF16, "pairs_last")
        back = [sb([P, T], F32, f"back{n}") for n in range(N_TILES)]

        for e in range(E):
            nc.vector.memset(w1s[e][:].bitcast(I32), 0)
        nc.vector.memset(w2s[:].rearrange("p e i -> p (e i)").bitcast(I32), 0)
        make_identity(nc, ident[:])
        for n in range(N_TILES):
            nc.gpsimd.memset(back[n][:], 0.0)

        def load_x(i):
            s, u, t0, t1 = LOADS[i][0], LOADS[i][1], LOADS[i][2], LOADS[i][5]
            rows = xT[s * P * PACK : (s + 1) * P * PACK, t0:t1]
            nc.sync.dma_start(
                out=xf[2 * s + u][:, :, t0:t1],
                in_=rows.rearrange("(p u e) t -> p u e t", u=2, e=2)[:, u, :, :],
            )

        def load_w1_scales(e, queue):
            rows = w1_scales[e].bitcast(I32).rearrange("s q i -> q s i")
            for r in range(4):
                queue.dma_start(
                    out=w1s[e][r:P:32, :].bitcast(I32).rearrange("q (s i) -> q s i", s=PASSES), in_=rows[r:16:4, :, :]
                )

        def load_w1(e, starts):
            for s0 in starts:
                tile = sb([P, 2, 2 * H], U8, f"w1_{e}_{s0}")
                nc.sync.dma_start(
                    out=tile[:].bitcast(I32), in_=w1_words[e, s0 : s0 + 2, :, :].bitcast(I32).rearrange("s p b -> p s b")
                )
                for s in range(s0, s0 + 2):
                    w1[e, s] = tile[:, s - s0, :]

        def load_w2_scales():
            rows = w2_scales[:, 0, :, :].bitcast(I32)
            for r in range(4):
                nc.sync.dma_start(
                    out=w2s[r:P:32, :, :].bitcast(I32),
                    in_=rows[:, r:16:4, :].rearrange("e q i -> q e i"),
                )

        def load_w2(e):
            nc.sync.dma_start(out=w2[e][:].bitcast(I32), in_=w2_words[e, 0, :, :].bitcast(I32))

        load_x(0)
        nc.sync.dma_start(offsets[:], offs)
        nc.sync.dma_start(out=gate_four[:], in_=gate[0, :].rearrange("(p f) -> p f", f=4))
        load_x(1)
        load_x(2)
        load_w1_scales(0, nc.sync)
        load_x(3)
        load_x(4)
        load_x(5)
        load_w2_scales()
        load_x(6)
        load_w1(0, [0])
        for i in range(7, len(LOADS)):
            load_x(i)
        load_w1_scales(1, nc.sync)
        load_w1(0, [2])
        load_w1(1, [0, 2])
        load_w2(0)
        load_w2(1)

        spread_gate = bank(4, [P, 4, P], "spread_gate")
        for f in range(4):
            nc.tensor.transpose(spread_gate[:, f, :], gate_four[:, f : f + 1].to_broadcast([P, P]), ident[:])
        nc.scalar.copy(out=gates[:].rearrange("q (p f) -> q p f", f=4), in_=spread_gate[:].rearrange("q f p -> q p f"))

        def cast(i):
            s, u, t0, cut0, cut1, t1 = LOADS[i]
            src = xf[2 * s + u][:].rearrange("p e t -> p t e")
            if t0 < cut0:
                nc.scalar.activation(pairs_of[s, u][:, t0:cut0, :], src[:, t0:cut0, :], COPY)
            if cut0 < cut1:
                nc.vector.tensor_copy(out=pairs_of[s, u][:, cut0:cut1, :], in_=src[:, cut0:cut1, :])
            if cut1 < t1:
                nc.gpsimd.tensor_copy(out=pairs_of[s, u][:, cut1:t1, :], in_=src[:, cut1:t1, :])

        def listed(lo, hi):
            return offsets[:, lo // 16 : hi // 16]

        def window(s, u):
            return pairs_of[s, u][:].rearrange("p t e -> p (t e)").bitcast(U32)

        codes = {}

        def quantise(s, lo, hi, woven):
            words = sb([P, hi - lo], U32, f"words{s}_{lo}")
            scales = sb([P, hi - lo], U8, f"scales{s}_{lo}")
            nc.vector.quantize_mx(out=words[:].bitcast(E4M3), scales=scales[:], in_=woven.bitcast(BF16))
            for g in range(lo // P, hi // P):
                cols = slice(g * P - lo, (g + 1) * P - lo)
                codes[s, g] = (words[:, cols], scales[:, cols])

        last = PASSES - 1
        for s in range(last):
            picked = sb([P, 2, S], U32, f"picked{s}")
            cast(2 * s)
            nc.vector.tensor_copy(picked[:, 0, :], window(s, 0).indirect(listed(0, S)))
            cast(2 * s + 1)
            for lo in (0, C):
                nc.vector.tensor_copy(picked[:, 1, lo : lo + C], window(s, 1).indirect(listed(lo, lo + C)))
            woven = sb([P, 2 * S], U32, f"woven{s}")
            for lo in (0, C):
                nc.vector.tensor_copy(
                    out=woven[:, 2 * lo : 2 * (lo + C)].rearrange("p (n u) -> p n u", u=2).bitcast(I32),
                    in_=picked[:, :, lo : lo + C].rearrange("p u n -> p n u").bitcast(I32),
                )
            for lo in (0, C):
                quantise(s, lo, lo + C, woven[:, 2 * lo : 2 * (lo + C)])

        cuts = [(0, P), (P, C)]
        final = [at(4096, [P, 2 * P], U32, "final0")[:], sb([P, 2 * P], U32, "final1")[:]]

        def pick(u, j):
            lo, hi = cuts[j]
            nc.vector.tensor_copy(
                final[j].rearrange("p (n u) -> p n u", u=2)[:, :, u], window(last, u).indirect(listed(lo, hi))
            )

        cast(2 * last)
        for j in range(len(cuts)):
            pick(0, j)
        for i in range(2 * last + 1, len(LOADS)):
            cast(i)
        pick(1, 0)
        pick(1, 1)
        quantise(last, 0, P, final[0])
        quantise(last, P, C, final[1])
        late = at(4096, [P, 2, C], U32, "late")
        nc.vector.tensor_copy(late[:, 0, :], window(last, 0).indirect(listed(C, S)))
        for lo in (0, P):
            nc.vector.tensor_copy(late[:, 1, lo : lo + P], window(last, 1).indirect(listed(C + lo, C + lo + P)))
        woven = sb([P, 2 * C], U32, "woven_late")
        for lo in (0, P):
            nc.vector.tensor_copy(
                out=woven[:, 2 * lo : 2 * (lo + P)].rearrange("p (n u) -> p n u", u=2).bitcast(I32),
                in_=late[:, :, lo : lo + P].rearrange("p u n -> p n u").bitcast(I32),
            )
        for lo in (0, P):
            quantise(last, C + lo, C + lo + P, woven[:, 2 * lo : 2 * (lo + P)])

        res = [at(offset, [P, T], F32, f"res{n}") for n, offset in enumerate((12288, 8192, 4096))]
        for n in (1, 0, 2):
            nc.sync.dma_start(out=res[n][:], in_=xr[n * P : (n + 1) * P, :])

        acc = {}

        def first(s, g):
            e = g // (C // P)
            nc.tensor.matmul_mx(
                out=acc[g][:],
                lhsT=codes[s, g][0].bitcast(E4M3),
                lhsT_scale=codes[s, g][1],
                rhs=w1[e, s].bitcast(E2M1),
                rhs_scale=w1s[e][:, s * H : (s + 1) * H],
                start=s == 0,
                stop=s == last,
            )

        h = {}
        hg = [sb([P, C, 2], F32, f"hg{e}") for e in range(E)]
        hq = [sb([P, C], U32, f"hq{e}") for e in range(E)]
        hs = [sb([P, C], U8, f"hs{e}") for e in range(E)]

        def activate(g):
            h[g] = sb([P, H], BF16, f"h{g}")
            dst = h[g][:].rearrange("p (w r e) -> p w r e", w=2, e=2)
            src = acc[g][:].rearrange("p (r w e) -> p w r e", w=2, e=2)
            nc.scalar.activation(dst, src, RELU)

        def turn(g):
            turned = bank(4 + g % 2, [P, 2, P], f"turned{g}")
            for w in range(2):
                nc.tensor.transpose(turned[:, w, :], h[g][:].bitcast(F32)[:, w * P : (w + 1) * P], ident[:])
            dst = hg[g // 2][:, g % 2 * P : (g % 2 + 1) * P, :]
            if g < 2:
                nc.scalar.copy(out=dst, in_=turned[:].rearrange("p w r -> p r w"))
            else:
                nc.vector.tensor_copy(out=dst, in_=turned[:].rearrange("p w r -> p r w"))

        def quantise_hidden(e, lo, hi):
            nc.vector.quantize_mx(
                out=hq[e][:, lo:hi].bitcast(E4M3),
                scales=hs[e][:, lo:hi],
                in_=hg[e][:, lo:hi, :].rearrange("p r w -> p (r w)").bitcast(BF16),
            )

        def second(e, n, lo, hi, dst):
            nc.tensor.matmul_mx(
                out=dst,
                lhsT=w2[e][:, 2 * P * n : 2 * P * (n + 1)].bitcast(E2M1),
                lhsT_scale=w2s[:, e, n * P : (n + 1) * P],
                rhs=hq[e][:, lo:hi].bitcast(E4M3),
                rhs_scale=hs[e][:, lo:hi],
                start=True,
                stop=True,
            )

        for g in range(GROUPS):
            acc[g] = bank(g, [P, H], f"acc{g}")

        def passes(e):
            for s in range(PASSES):
                first(s, 2 * e)
                first(s, 2 * e + 1)

        passes(0)
        def results(b, parts):
            sums = bank(b, [P, sum(hi - lo for n, lo, hi, gated in parts)], "y%d_%d" % parts[0][:2])
            at_col = 0
            for n, lo, hi, gated in parts:
                e = lo // C
                second(e, n, lo - e * C, hi - e * C, sums[:, at_col : at_col + hi - lo])
                at_col = at_col + hi - lo
            at_col = 0
            for n, lo, hi, gated in parts:
                nc.vector.tensor_tensor(gated, sums[:, at_col : at_col + hi - lo], gates[:, lo:hi], MULT)
                at_col = at_col + hi - lo

        def result(n, lo, hi, b, gated):
            results(b, [(n, lo, hi, gated)])

        def scatter(n, lo, hi, gated):
            if n == 1:
                nc.vector.tensor_copy(back[n][:].indirect(listed(lo, hi)), gated)
            else:
                nc.scalar.activation(back[n][:].indirect(listed(lo, hi)), gated, COPY)

        gated0 = sb([P, S], F32, "gated0")
        gated2 = sb([P, S], F32, "gated2")
        gated1 = [sb([P, P], F32, "gated1_0"), at(0, [P, S - P], F32, "gated1_1")]
        activate(0)
        activate(1)
        turn(0)
        turn(1)
        quantise_hidden(0, 0, P)
        result(1, 0, P, 6, gated1[0][:])
        quantise_hidden(0, P, C)
        scatter(1, 0, P, gated1[0][:])
        passes(1)
        activate(2)
        activate(3)
        result(0, 0, C, 2, gated0[:, 0:C])
        scatter(0, 0, C, gated0[:, 0:C])
        turn(2)
        turn(3)
        quantise_hidden(1, 0, C)
        results(5, [(2, 0, C, gated2[:, 0:C]), (1, P, C, gated1[1][:, 0:P])])
        scatter(2, 0, P, gated2[:, 0:P])
        result(0, C, S, 0, gated0[:, C:S])
        scatter(0, C, S, gated0[:, C:S])
        result(1, C, S, 7, gated1[1][:, P:])
        result(2, C, S, 1, gated2[:, C:S])
        scatter(2, P, S, gated2[:, P:S])
        scatter(1, P, S, gated1[1][:])

        def add(engine, n, lo, hi, dst):
            engine.tensor_tensor(dst, back[n][:, lo:hi], res[n][:, lo:hi], ADD)
            nc.sync.dma_start(out=out[n * P : (n + 1) * P, lo:hi], in_=dst)

        sums = sb([P, T], F32, "sums")
        add(nc.gpsimd, 0, 0, 512, back[0][:, 0:512])
        for lo in range(0, T, 512):
            add(nc.vector, 1, lo, lo + 512, sums[:, lo : lo + 512])
        add(nc.vector, 0, 512, T, back[1][:, 0:512])
        for lo, hi in ((0, 512), (512, 768), (768, T)):
            add(nc.vector, 2, lo, hi, res[1][:, lo:hi])
